import numpy as np, ml_dtypes
CORES = [2,3,42,43,82,83,122,123]
N = 8
BF = ml_dtypes.bfloat16
def f(rng, *shape):
    return (rng.standard_normal(shape, dtype=np.float32) * np.exp2(rng.integers(-2, 3, shape[:-1] + (1,)))).astype(BF)
def wide(rng, *shape):
    v = f(rng, *shape).astype(np.float32); k = shape[:-2] + (1, shape[-1])
    return (v * np.exp2(rng.integers(-6, 7, k)) * (rng.random(k) > 0.0625)).astype(BF)
R, W, S, C = 8, 64, 4, 2
H = N * R
ROW, COL = np.arange(H)[None, :, None], np.arange(W)[None, None, :]
def stored(v):
    return np.ascontiguousarray(v.reshape(8, N, R, W).transpose(1, 0, 2, 3)).reshape(N, 8, R * W).astype(np.int32)
def whole(v):
    return np.ascontiguousarray(v.reshape(N, 8, R, W).transpose(1, 0, 2, 3)).reshape(8, H, W).astype(np.int64)
def field(rng):
    d = np.repeat(np.repeat(rng.integers(-1, 2, (2, 8, H // 8, W // 16)), 8, axis=2), 16, axis=3)
    d = np.roll(d, int(rng.integers(1, 8)), axis=2)
    return np.where(rng.random(d.shape) < 0.125, rng.integers(-1, 2, d.shape), d)
def inputs_of(rng, v):
    return {"vy": stored(v[0]), "vx": stored(v[1]), "img": f(rng, N, 128, C * R * W)}
def setup_inputs(rng):
    return inputs_of(rng, field(rng))
def setup_inputs_far(rng):
    v = np.zeros((2, 8, H, W), np.int64); o = rng.permutation(8)
    for k in range(8):
        v[0, o[k]] = 1 if k & 1 else -1; v[1, o[k]] = 1 if k & 2 else -1
        if k >= 4:
            m = rng.random((2, H, W)) < 0.015625
            v[:, o[k]] = np.where(m, rng.integers(-1, 2, (2, H, W)), v[:, o[k]])
    return inputs_of(rng, v)
def setup_inputs_ends(rng):
    v = field(rng); pm = np.array([-1, 1])
    for e in (0, H - 1): v[0, :, e, :] = rng.choice(pm, (8, W))
    for e in (0, W - 1): v[1, :, :, e] = rng.choice(pm, (8, H))
    v[0, :, 1, :] = np.where(rng.random((8, W)) < 0.75, -1, 1); v[0, :, H - 2, :] = np.where(rng.random((8, W)) < 0.75, 1, -1)
    v[1, :, :, 1] = np.where(rng.random((8, H)) < 0.75, -1, 1); v[1, :, :, W - 2] = np.where(rng.random((8, H)) < 0.75, 1, -1)
    o = rng.permutation(8); g, h = o[0], o[1]
    v[0, g, 0, :] = 2 * (np.arange(W) & 1) - 1; v[1, g, 0, :] = 1
    v[0, g, H - 1, :] = 2 * (np.arange(W) & 1) - 1; v[1, g, H - 1, :] = -1
    v[1, h, :, 0] = 2 * (np.arange(H) & 1) - 1; v[0, h, :, 0] = 1
    v[1, h, :, W - 1] = 2 * (np.arange(H) & 1) - 1; v[0, h, :, W - 1] = -1
    return inputs_of(rng, v)
def setup_inputs_sinks(rng):
    v = np.zeros((2, 8, H, W), np.int64); o = rng.permutation(8)
    v[1, o[1]] = 1 - 2 * (COL[0] & 1)
    v[0, o[2]] = 2 * (ROW[0] & 1) - 1
    for k in range(3, 8):
        r0, c0 = int(rng.integers(0, H)), int(rng.integers(0, W))
        if k == 3: r0 = R * int(rng.integers(1, N))
        if k == 4: r0 = R * int(rng.integers(1, N)) - 1
        v[0, o[k]] = np.sign(r0 - ROW[0]); v[1, o[k]] = np.sign(c0 - COL[0])
    return inputs_of(rng, v)
def setup_inputs_spread(rng):
    d = setup_inputs(rng); d["img"] = wide(rng, N, 128, C * R * W); return d
def check_inputs(d):
    bad = [k for k in ("vy", "vx") if not np.isin(np.asarray(d[k]), [-1, 0, 1]).all()]
    return bad + ([] if np.isfinite(np.asarray(d["img"]).astype(np.float32)).all() else ["finite"])
def place(a, b):
    return np.minimum(np.maximum(ROW + a, 0), H - 1), (COL + b) % W
def reference(vy, vx, img):
    a, b = whole(vy), whole(vx); g = np.arange(8)[:, None, None]
    for s in range(S):
        p, q = place(a, b)
        a, b = a + a[g, p, q], b + b[g, p, q]
    p, q = place(a, b)
    u = np.ascontiguousarray(img.reshape(N, 8, 16, C, R, W).transpose(1, 0, 4, 5, 2, 3)).reshape(8, H, W, 16, C)
    z = u[g, p, q].reshape(8, N, R, W, 16, C)
    return {"y": np.ascontiguousarray(z.transpose(1, 0, 4, 5, 2, 3)).reshape(N, 128, C * R * W)}

@@ -1,0 +1,372 @@
+from concourse.bass import DstId, RemoteDMATransfer
+from concourse.mybir import AluOpType, ActivationFunctionType
+
+ROWS = 40
+SCRATCH = {
+    "vraw": ("sbuf", [128, 64], "int32"),
+    "xs": ("sbuf", [128, 64], "int32"),
+    "xm": ("sbuf", [128, 64], "int32"),
+    "lland": ("sbuf", [128, 5 * 32], "uint16"),
+    "vland": ("sbuf", [128, 5 * 64], "bfloat16"),
+    "xio": ("sbuf", [128, 64], "int32"),
+    "kidx": ("sbuf", [128, 1], "int32"),
+    "k7": ("sbuf", [128, 1], "int32"),
+    "k8": ("sbuf", [128, 1], "int32"),
+    "k16": ("sbuf", [128, 1], "int32"),
+    "cols": ("sbuf", [128, 16], "float32"),
+    "qio": ("sbuf", [128, 128], "bfloat16"),
+    "zio": ("sbuf", [128, 144], "bfloat16"),
+    "lx": ("sbuf", [128, 8 * 128], "bfloat16"),
+    "z": ("sbuf", [128, 144], "bfloat16"),
+    "f0": ("sbuf", [128, ROWS * 64], "bfloat16"),
+    "f1": ("sbuf", [128, ROWS * 64], "bfloat16"),
+    "f2": ("sbuf", [128, ROWS * 64], "bfloat16"),
+    "f3": ("sbuf", [128, ROWS * 64], "bfloat16"),
+    "f4": ("sbuf", [128, 512], "bfloat16"),
+    "l0": ("sbuf", [128, ROWS * 4], "uint16"),
+    "l1": ("sbuf", [128, ROWS * 4], "uint16"),
+    "l2": ("sbuf", [128, ROWS * 4], "uint16"),
+    "l3": ("sbuf", [128, ROWS * 4], "uint16"),
+    "l4": ("sbuf", [128, 32], "uint16"),
+    "ca": ("sbuf", [128, 32], "int32"),
+    "cb": ("sbuf", [128, 32], "int32"),
+    "cc": ("sbuf", [128, 32], "int32"),
+    "pic": ("sbuf", [128, 5 * 1024], "bfloat16"),
+    "yo": ("sbuf", [128, 1024], "bfloat16"),
+    "ps": ("psum", [128, 8 * 512], "float32"),
+}
+SEMAPHORES = (["ve", "ac", "pe", "gp", "ldy", "ldx", "ldi", "sta", "stb", "lv", "ll", "li", "lf"]
+              + ["va%d" % k for k in range(5)] + ["la%d" % k for k in range(5)] + ["ia%d" % k for k in range(5)])
+OP = AluOpType
+COPY, IDENT = ActivationFunctionType.Copy, ActivationFunctionType.Identity
+
+
+def bits(engines):
+    return sum(1 << e for e in engines)
+
+
+def rank_program(g, core, T, topo):
+    r = T.rank_of(core)
+    if r is None:
+        return
+    cores = list(T.cores)
+    n = len(cores)
+    S = T.sem
+    queues = {"ve": g.vector, "ac": g.scalar, "pe": g.tensor, "gp": g, "sy": g.sync}
+    done = {"ve": 0, "ac": 0, "pe": 0, "gp": 0}
+    seen = {q: {} for q in queues}
+
+    def need(q, deps):
+        best = {}
+        for s, v in deps:
+            best[s] = max(best.get(s, 0), v)
+        for s, v in best.items():
+            if seen[q].get(s, 0) < v:
+                queues[q].wait_ge(S[s], v)
+                seen[q][s] = v
+
+    def mark(q, ins):
+        ins.then_inc(S[q], 1)
+        done[q] += 1
+        return (q, done[q])
+
+    def vec(name, deps, *args):
+        need("ve", deps)
+        f = {"ts": g.vector.tensor_scalar, "tt": g.vector.tensor_tensor, "tc": g.vector.tensor_copy}[name]
+        return mark("ve", f(*args))
+
+    def act(deps, out, in_, func, **kw):
+        need("ac", deps)
+        return mark("ac", g.scalar.activation(out, in_, func, **kw))
+
+    tabs = [T.f0, T.f1, T.f2, T.f3, T.f4]
+    lists = [T.l0, T.l1, T.l2, T.l3]
+    wrote = [[], [], [], [], []]
+    listed = [[], [], [], []]
+
+    def toks(book, a, b):
+        return [t for lo, hi, t in book if lo < b and a < hi]
+
+    g.sync.dma_start(T.vraw[0:64, :], T.vy[:, :]).then_inc(S.ldy, 16)
+    g.scalar.dma_start(T.vraw[64:128, :], T.vx[:, :]).then_inc(S.ldx, 16)
+    g.sync.dma_start(T.pic[:, 2 * 1024:3 * 1024], T.img[:, :]).then_inc(S.ldi, 16)
+
+    t_k = mark("gp", g.iota(T.kidx[:, :], [[1, 1]], 0, 1))
+    t_x = mark("gp", g.iota(T.xio[:, :], [[1, 64]], 0, 0))
+    t_q = mark("gp", g.iota(T.qio[:, :], [[8, 8], [64, 2], [0, 8]], 0, 0, allow_small_or_imprecise_dtypes=True))
+    t_zi = mark("gp", g.iota(T.zio[:, :], [[1, 144]], -15, 0, allow_small_or_imprecise_dtypes=True))
+
+    def col(j):
+        return T.cols[:, j:j + 1]
+    a = vec("ts", [t_k], T.k7[:, :], T.kidx[:, :], 7, None, OP.bitwise_and)
+    b8 = vec("ts", [], T.k8[:, :], T.kidx[:, :], 8, None, OP.bitwise_and)
+    c16 = vec("ts", [], T.k16[:, :], T.kidx[:, :], 112, None, OP.bitwise_and)
+    t_kf = vec("tc", [], col(1), T.kidx[:, :])
+    t_row = vec("ts", [a], col(0), T.k7[:, :], float(8 * r), None, OP.add)
+    base = 16 - 8 * r
+    t_d = vec("ts", [b8], col(2), T.k8[:, :], -base / 8.0, float(base), OP.mult, OP.add)
+    t_w = vec("ts", [b8], col(3), T.k8[:, :], -0.984375, 8.0, OP.mult, OP.add)
+    t_16 = vec("tc", [c16], col(4), T.k16[:, :])
+    wl = base if base > 0 else None
+    wh = base + 8 * n - 1 if base + 8 * n - 1 < ROWS - 1 else None
+    side = -1 if wl is not None else 1
+    edge = wl if wl is not None else wh
+    t_pad, t_clo, t_chi = {}, None, None
+    t_L = [vec("ts", [t_q, t_kf], T.lx[:, i * 128:(i + 1) * 128], T.qio[:, :], float(i), col(1), OP.add, OP.is_equal)
+           for i in range(8)]
+    t_z = vec("ts", [t_zi, t_16, t_w], T.z[:, :], T.zio[:, :], col(4), col(3), OP.is_equal, OP.mult)
+    if edge is not None:
+        for j, k in enumerate((1, 2, 4, 8)):
+            t_pad[k] = vec("ts", [b8], col(5 + j), T.k8[:, :], -side * k / 8.0, float(side * k), OP.mult, OP.add)
+        lo_v = wl if wl is not None else 0
+        hi_v = wh if wh is not None else ROWS - 1
+        t_clo = vec("ts", [b8], col(9), T.k8[:, :], -lo_v / 8.0, float(lo_v), OP.mult, OP.add)
+        t_chi = vec("ts", [b8], col(10), T.k8[:, :], (255 - hi_v) / 8.0, float(hi_v), OP.mult, OP.add)
+    padcol = {1: 5, 2: 6, 4: 7, 8: 8}
+
+    own = slice(2 * 64, 3 * 64)
+    need("ve", [("ldx", 16)])
+    x1 = vec("tt", [t_x], T.xs[64:128, :], T.vraw[64:128, :], T.xio[64:128, :], OP.add)
+    need("ve", [("ldy", 16)])
+    ty = vec("ts", [t_row], T.vland[0:64, own], T.vraw[0:64, :], T.cols[0:64, 0:1], None, OP.add)
+    x2 = vec("ts", [x1], T.xm[64:128, :], T.xs[64:128, :], 63, None, OP.bitwise_and)
+    tx = vec("tc", [x2], T.vland[64:128, own], T.xm[64:128, :])
+
+    near = [t for t in range(n) if t != r and abs(t - r) <= 2]
+
+    def same(t):
+        return topo.chip(cores[t]) == topo.chip(core)
+    off, on = [t for t in near if not same(t)], [t for t in near if same(t)]
+    mate = on[0]
+    far = [t for t in near if abs(t - r) == 2]
+    e_off = topo.engines(core, cores[off[0]])
+    e_all = [e for e in topo.engines(core, cores[mate]) if e not in e_off]
+    e_on = e_all[:4]
+
+    def sname(kind, sender):
+        return "%s%d" % (kind, sender % 5)
+
+    def transfer(buf, width, kind, sender, targets, engines):
+        k = sender - r + 2
+        ids = []
+        for t in targets:
+            rid, pid, _ = topo.addr(cores[t])
+            ids.append(DstId(rid=rid, pnc=pid))
+        return RemoteDMATransfer(dst_ids=ids, dma_engine_mask=bits(engines), remote_sem=S[sname(kind, sender)],
+                                 srcs=[buf[:, k * width:(k + 1) * width]],
+                                 dsts=[buf[:, (sender - t + 2) * width:(sender - t + 3) * width] for t in targets])
+
+    need("gp", [ty, tx])
+    g.remote_dma_fused([transfer(T.vland, 64, "va", r, on, e_on), transfer(T.vland, 64, "va", r, off, e_off)],
+                       local_sem=S.lv)
+
+    T0 = T.f0
+    slots = [k for k in range(5) if 0 <= r + k - 2 < n]
+    first0, end0 = 8 * slots[0], 8 * slots[-1] + 8
+    if wl is not None:
+        first0 = wl - 1
+    if wh is not None:
+        end0 = wh + 2
+    ps_free = {}
+    turn = [0]
+
+    def spread(k):
+        if k == 2:
+            need("pe", t_L + [ty, tx])
+        else:
+            t = r + k - 2
+            need("pe", [(sname("va", t), len(e_on) if same(t) else len(e_off))])
+        for h in range(2):
+            bank = (2 * turn[0] + h) % 8
+            need("pe", ps_free.get(bank, []))
+            for j in range(4):
+                i = 4 * h + j
+                t = mark("pe", g.tensor.matmul(T.ps[:, bank * 512 + j * 64:bank * 512 + j * 64 + 64],
+                                               T.lx[:, i * 128:(i + 1) * 128], T.vland[:, k * 64:k * 64 + 64], True, True))
+            out, src = T0[:, k * 512 + h * 256:k * 512 + h * 256 + 256], T.ps[:, bank * 512:bank * 512 + 256]
+            if h == 0:
+                v = vec("ts", [t, t_d], out, src, col(2), None, OP.add)
+            else:
+                v = act([t, t_d], out, src, IDENT, bias=col(2))
+            wrote[0].append((8 * k + 4 * h, 8 * k + 4 * h + 4, v))
+            ps_free[bank] = [v]
+        turn[0] += 1
+
+    def pads(s, want):
+        have = 1
+        while have <= want:
+            m = min(have, want + 1 - have)
+            if side < 0:
+                d0, s0 = edge - have - m + 1, edge - m + 1
+            else:
+                d0, s0 = edge + have, edge
+            v = vec("ts", toks(wrote[s], s0, s0 + m) + [t_pad[have]], tabs[s][:, d0 * 64:(d0 + m) * 64],
+                    tabs[s][:, s0 * 64:(s0 + m) * 64], col(padcol[have]), None, OP.add)
+            wrote[s].append((d0, d0 + m, v))
+            have += m
+
+    def pick(s, a, b, bank):
+        cells = (b - a) * 64
+        need("pe", toks(wrote[s], a, b) + ps_free.get(bank, []) + [t_z])
+        for k in range(16):
+            t = mark("pe", g.tensor.matmul(T.ps[:, bank * 512:bank * 512 + cells // 16], T.z[:, 15 - k:143 - k],
+                                           tabs[s][:, a * 64 + k:b * 64:16], k == 0, k == 15))
+        return t
+
+    def note(s, a, b, bank, t, wbase):
+        v = vec("ts", [t], lists[s][:, a * 4:b * 4], T.ps[:, bank * 512:bank * 512 + (b - a) * 4], float(-64 * wbase),
+                None, OP.add)
+        listed[s].append((a, b, v))
+        ps_free[bank] = [v]
+
+    def look(q, s, a, b, win):
+        if a >= b:
+            return
+        o = 16 if s == 3 else 0
+        src = tabs[s][:, win[0] * 64:win[1] * 64].indirect(lists[s][:, a * 4:b * 4])
+        out = tabs[s + 1][:, (a - o) * 64:(b - o) * 64]
+        deps = toks(wrote[s], win[0], win[1]) + toks(listed[s], a, b)
+        if q == "ve":
+            if s == 3 and edge is not None:
+                v = vec("ts", deps + [t_clo, t_chi], out, src, col(9), col(10), OP.max, OP.min)
+            else:
+                v = vec("tc", deps, out, src)
+        else:
+            v = act(deps, out, src, COPY)
+            if s == 3 and edge is not None:
+                v = vec("ts", [v, t_clo, t_chi], out, out, col(9), col(10), OP.max, OP.min)
+        wrote[s + 1].append((a, b, v))
+
+    def both(s, a, b, win):
+        if a >= b:
+            return
+        m = (a + b) // 2
+        if edge is not None and edge >= m:
+            look("ac", s, a, m, win)
+            look("ve", s, m, b, win)
+        else:
+            look("ac", s, m, b, win)
+            look("ve", s, a, m, win)
+
+    def real(a, b):
+        return max(a, wl if wl is not None else a), min(b, wh + 1 if wh is not None else b)
+
+    spread(2)
+    tp = pick(0, 16, 24, 6)
+    tl = vec("ts", [tp], T.lland[:, 64:96], T.ps[:, 6 * 512:6 * 512 + 32], float(64 * (1 - base)), None, OP.add)
+    need("gp", [tl])
+    g.remote_dma_fused([transfer(T.lland, 32, "la", r, on, e_on), transfer(T.lland, 32, "la", r, off, e_off)],
+                       local_sem=S.ll)
+    g.wait_ge(S.ldi, 16)
+    g.remote_dma_fused([transfer(T.pic, 1024, "ia", r, far, e_off), transfer(T.pic, 1024, "ia", r, [mate], e_all)],
+                       local_sem=S.li)
+    passed = r + 2 if mate > r else r - 2
+    n_f = 0
+    if 0 <= passed < n:
+        g.wait_ge(S[sname("ia", passed)], len(e_off))
+        rid, pid, _ = topo.addr(cores[mate])
+        k = passed - r + 2
+        g.remote_dma(T.pic[:, (passed - mate + 2) * 1024:(passed - mate + 3) * 1024], T.pic[:, k * 1024:(k + 1) * 1024],
+                     S[sname("ia", passed)], S.lf, pid, rid, bits(e_all))
+        n_f = len(e_all)
+
+    if edge in (16, 23):
+        pads(0, 1)
+    wide0 = {"own": (max(8, first0), min(32, end0)), "low": (first0, 24), "high": (16, end0)}
+    note(0, 16, 24, 6, tp, wide0["own"][0])
+    lowrows, highrows = real(2, 16), real(24, 38)
+
+    def fetch(k, a, b, wbase):
+        t = r + k - 2
+        need("ve", [(sname("la", t), len(e_on) if same(t) else len(e_off))])
+        v = vec("ts", [], lists[0][:, a * 4:b * 4], T.lland[:, 32 * k + (a - 8 * k) * 4:32 * k + (b - 8 * k) * 4],
+                float(-64 * (1 - base) - 64 * wbase), None, OP.add)
+        listed[0].append((a, b, v))
+
+    for k in sorted([k for k in (1, 3) if k in slots], key=lambda k: not same(r + k - 2)):
+        spread(k)
+        if edge in (8, 31) and edge // 8 == k:
+            pads(0, 1)
+    both(0, 16, 24, wide0["own"])
+    for k, rows, name in ((0, lowrows, "low"), (4, highrows, "high")):
+        if rows[0] >= rows[1]:
+            continue
+        if k in slots:
+            spread(k)
+        for q in (1, 0) if k == 0 else (3, 4):
+            if q in slots:
+                fetch(q, max(rows[0], 8 * q), min(rows[1], 8 * q + 8), wide0[name][0])
+        both(0, rows[0], rows[1], wide0[name])
+
+    def window(lo, hi, reach):
+        a, b = real(lo, hi)
+        if wl is not None:
+            a = max(lo, wl - reach)
+        if wh is not None:
+            b = min(hi, wh + 1 + reach)
+        return a, b
+
+    w1, w2, w3 = window(2, 38, 2), window(4, 36, 4), window(8, 32, 8)
+
+    def finish(s, win):
+        if wl is not None and win[0] < wl:
+            pads(s, wl - win[0])
+        if wh is not None and win[1] > wh + 1:
+            pads(s, win[1] - wh - 1)
+
+    a, b = real(4, 24)
+    tp = pick(1, a, b, 0)
+    finish(1, w1)
+    note(1, a, b, 0, tp, w1[0])
+    c, d = real(24, 36)
+    if c < d:
+        tp2 = pick(1, c, d, 1)
+    both(1, a, b, w1)
+    if c < d:
+        note(1, c, d, 1, tp2, w1[0])
+        both(1, c, d, w1)
+    a, b = real(8, 24)
+    tp = pick(2, a, b, 2)
+    finish(2, w2)
+    note(2, a, b, 2, tp, w2[0])
+    c, d = real(24, 32)
+    if c < d:
+        tp2 = pick(2, c, d, 3)
+    both(2, 16, 24, w2)
+    tp3 = pick(3, 16, 24, 4)
+    both(2, a, min(b, 16), w2)
+    if c < d:
+        note(2, c, d, 3, tp2, w2[0])
+        both(2, c, d, w2)
+    finish(3, w3)
+    note(3, 16, 24, 4, tp3, w3[0])
+    both(3, 16, 24, w3)
+
+    need("pe", toks(wrote[4], 16, 24) + ps_free.get(5, []))
+    for k in range(16):
+        tp = mark("pe", g.tensor.matmul(T.ps[:, 5 * 512:5 * 512 + 32], T.z[:, 15 - k:143 - k], T.f4[:, k:512:16],
+                                        k == 0, k == 15))
+    v = vec("tc", [tp], T.ca[:, :], T.ps[:, 5 * 512:5 * 512 + 32])
+    v = vec("ts", [v], T.cb[:, :], T.ca[:, :], 0xE00, None, OP.bitwise_and)
+    v = vec("tt", [v], T.cc[:, :], T.ca[:, :], T.cb[:, :], OP.add)
+    v = vec("ts", [v], T.l4[:, :], T.cc[:, :], float(-1024 * slots[0]), None, OP.add)
+    arrived = [(sname("ia", t), len(e_off) if t in far else len(e_all)) for t in near] + [("ldi", 16)]
+    c0, c1 = slots[0] * 1024, slots[-1] * 1024 + 1024
+    need("ve", arrived)
+    need("ac", arrived)
+    va = vec("tc", [v], T.yo[:, 0:512], T.pic[:, c0:c1 - 512].indirect(T.l4[:, :]))
+    vb = act([v], T.yo[:, 512:1024], T.pic[:, c0 + 512:c1].indirect(T.l4[:, :]), COPY)
+    need("sy", [va])
+    g.sync.dma_start(T.y[:, 0:512], T.yo[:, 0:512]).then_inc(S.sta, 16)
+    need("ac", [vb])
+    g.scalar.dma_start(T.y[:, 512:1024], T.yo[:, 512:1024]).then_inc(S.stb, 16)
+    g.sync.wait_ge(S.sta, 16)
+    g.scalar.wait_ge(S.stb, 16)
+    g.wait_ge(S.lv, len(e_off) + len(e_on))
+    g.wait_ge(S.ll, len(e_off) + len(e_on))
+    g.wait_ge(S.li, len(e_off) + len(e_all))
+    if n_f:
+        g.wait_ge(S.lf, n_f)
+    for q in ("ve", "ac", "pe"):
+        g.wait_ge(S[q], done[q])
+    g.wait_ge(S.gp, done["gp"])

@@ -1,23 +1,24 @@
 from concourse.bass import DstId, RemoteDMATransfer
 from concourse.mybir import AluOpType, ActivationFunctionType
 
+HELP = 320
+HELP_ENGINES = 4
 ROWS = 40
 SCRATCH = {
     "vraw": ("sbuf", [128, 64], "int32"),
-    "xs": ("sbuf", [128, 64], "int32"),
-    "xm": ("sbuf", [128, 64], "int32"),
-    "lland": ("sbuf", [128, 5 * 32], "uint16"),
+    "ioc": ("sbuf", [128, 64], "int32"),
     "vland": ("sbuf", [128, 5 * 64], "bfloat16"),
-    "xio": ("sbuf", [128, 64], "int32"),
     "kidx": ("sbuf", [128, 1], "int32"),
+    "k1": ("sbuf", [128, 1], "int32"),
     "k7": ("sbuf", [128, 1], "int32"),
-    "k8": ("sbuf", [128, 1], "int32"),
+    "k15": ("sbuf", [128, 1], "int32"),
     "k16": ("sbuf", [128, 1], "int32"),
-    "cols": ("sbuf", [128, 16], "float32"),
+    "cols": ("sbuf", [128, 32], "float32"),
     "qio": ("sbuf", [128, 128], "bfloat16"),
     "zio": ("sbuf", [128, 144], "bfloat16"),
     "lx": ("sbuf", [128, 8 * 128], "bfloat16"),
     "z": ("sbuf", [128, 144], "bfloat16"),
+    "z4": ("sbuf", [128, 144], "bfloat16"),
     "f0": ("sbuf", [128, ROWS * 64], "bfloat16"),
     "f1": ("sbuf", [128, ROWS * 64], "bfloat16"),
     "f2": ("sbuf", [128, ROWS * 64], "bfloat16"),
@@ -28,26 +29,57 @@ SCRATCH = {
     "l2": ("sbuf", [128, ROWS * 4], "uint16"),
     "l3": ("sbuf", [128, ROWS * 4], "uint16"),
     "l4": ("sbuf", [128, 32], "uint16"),
-    "ca": ("sbuf", [128, 32], "int32"),
-    "cb": ("sbuf", [128, 32], "int32"),
-    "cc": ("sbuf", [128, 32], "int32"),
     "pic": ("sbuf", [128, 5 * 1024], "bfloat16"),
+    "part": ("sbuf", [128, HELP], "bfloat16"),
     "yo": ("sbuf", [128, 1024], "bfloat16"),
     "ps": ("psum", [128, 8 * 512], "float32"),
 }
-SEMAPHORES = (["ve", "ac", "pe", "gp", "ldy", "ldx", "ldi", "sta", "stb", "lv", "ll", "li", "lf"]
-              + ["va%d" % k for k in range(5)] + ["la%d" % k for k in range(5)] + ["ia%d" % k for k in range(5)])
+SEMAPHORES = (["ve", "ac", "pe", "gp", "ldy", "ldx", "ldi", "sta", "lv", "li", "lf", "lh", "hi", "hl"]
+              + [k + str(j) for k in ("va", "ia", "h") for j in range(5)])
 OP = AluOpType
-COPY, IDENT = ActivationFunctionType.Copy, ActivationFunctionType.Identity
+COPY, IDENT, RELU = ActivationFunctionType.Copy, ActivationFunctionType.Identity, ActivationFunctionType.Relu
 
 
 def bits(engines):
     return sum(1 << e for e in engines)
 
 
+def address(topo, c):
+    rid, pid, _ = topo.addr(c)
+    return DstId(rid=rid, pnc=pid)
+
+
+def outside(T, topo, r):
+    n = len(T.cores)
+    there = [t for t in range(n) if abs(t - r) <= 2 and topo.chip(T.cores[t]) != topo.chip(T.cores[r])]
+    return sorted(there, key=lambda t: (abs(t - r), min(t, n - 1 - t)))
+
+
+def helper(T, topo, r):
+    me = T.cores[r]
+    here = [c for c in T.cores if topo.chip(c) == topo.chip(me)]
+    free = [c for c in topo.cores_of(me) if c not in T.cores and topo.die(c) != topo.die(me)
+            and all(topo.may_write(c, T.cores[t]) for t in outside(T, topo, r))]
+    return free[here.index(me)]
+
+
+def relay(g, core, T, topo, r):
+    off = outside(T, topo, r)
+    es = topo.engines(core, T.cores[off[0]])
+    g.wait_ge(T.sem.hi, HELP_ENGINES)
+    g.remote_dma_fused([RemoteDMATransfer(
+        dst_ids=[address(topo, T.cores[t]) for t in off], dma_engine_mask=bits(es), remote_sem=T.sem["h%d" % (r % 5)],
+        srcs=[T.part[:, :]], dsts=[T.pic[:, (r - t + 3) * 1024 - HELP:(r - t + 3) * 1024] for t in off])],
+        local_sem=T.sem.hl)
+    g.wait_ge(T.sem.hl, len(es))
+
+
 def rank_program(g, core, T, topo):
     r = T.rank_of(core)
     if r is None:
+        for r in range(len(T.cores)):
+            if helper(T, topo, r) == core:
+                relay(g, core, T, topo, r)
         return
     cores = list(T.cores)
     n = len(cores)
@@ -92,53 +124,42 @@ def rank_program(g, core, T, topo):
     g.sync.dma_start(T.pic[:, 2 * 1024:3 * 1024], T.img[:, :]).then_inc(S.ldi, 16)
 
     t_k = mark("gp", g.iota(T.kidx[:, :], [[1, 1]], 0, 1))
-    t_x = mark("gp", g.iota(T.xio[:, :], [[1, 64]], 0, 0))
+    t_x = mark("gp", g.iota(T.ioc[:, :], [[1, 64]], 0, 0))
     t_q = mark("gp", g.iota(T.qio[:, :], [[8, 8], [64, 2], [0, 8]], 0, 0, allow_small_or_imprecise_dtypes=True))
     t_zi = mark("gp", g.iota(T.zio[:, :], [[1, 144]], -15, 0, allow_small_or_imprecise_dtypes=True))
 
     def col(j):
         return T.cols[:, j:j + 1]
-    a = vec("ts", [t_k], T.k7[:, :], T.kidx[:, :], 7, None, OP.bitwise_and)
-    b8 = vec("ts", [], T.k8[:, :], T.kidx[:, :], 8, None, OP.bitwise_and)
+    c = col(11)
+    k7 = vec("ts", [t_k], T.k7[:, :], T.kidx[:, :], 7, None, OP.bitwise_and)
+    c15 = vec("ts", [], T.k15[:, :], T.kidx[:, :], 15, None, OP.bitwise_and)
+    t_row = vec("ts", [k7], col(0), T.k7[:, :], float(8 * r), None, OP.add)
     c16 = vec("ts", [], T.k16[:, :], T.kidx[:, :], 112, None, OP.bitwise_and)
+    t_r = vec("ts", [t_row, t_x], T.ioc[0:64, :], T.ioc[0:64, :], 0.0, T.cols[0:64, 0:1], OP.mult, OP.add)
     t_kf = vec("tc", [], col(1), T.kidx[:, :])
-    t_row = vec("ts", [a], col(0), T.k7[:, :], float(8 * r), None, OP.add)
-    base = 16 - 8 * r
-    t_d = vec("ts", [b8], col(2), T.k8[:, :], -base / 8.0, float(base), OP.mult, OP.add)
-    t_w = vec("ts", [b8], col(3), T.k8[:, :], -0.984375, 8.0, OP.mult, OP.add)
+    t_15 = vec("tc", [c15], c, T.k15[:, :])
     t_16 = vec("tc", [c16], col(4), T.k16[:, :])
+    t_1 = vec("ts", [], T.k1[:, :], T.kidx[:, :], 1, None, OP.bitwise_and)
+    base = 16 - 8 * r
     wl = base if base > 0 else None
     wh = base + 8 * n - 1 if base + 8 * n - 1 < ROWS - 1 else None
     side = -1 if wl is not None else 1
     edge = wl if wl is not None else wh
-    t_pad, t_clo, t_chi = {}, None, None
-    t_L = [vec("ts", [t_q, t_kf], T.lx[:, i * 128:(i + 1) * 128], T.qio[:, :], float(i), col(1), OP.add, OP.is_equal)
-           for i in range(8)]
-    t_z = vec("ts", [t_zi, t_16, t_w], T.z[:, :], T.zio[:, :], col(4), col(3), OP.is_equal, OP.mult)
-    if edge is not None:
-        for j, k in enumerate((1, 2, 4, 8)):
-            t_pad[k] = vec("ts", [b8], col(5 + j), T.k8[:, :], -side * k / 8.0, float(side * k), OP.mult, OP.add)
-        lo_v = wl if wl is not None else 0
-        hi_v = wh if wh is not None else ROWS - 1
-        t_clo = vec("ts", [b8], col(9), T.k8[:, :], -lo_v / 8.0, float(lo_v), OP.mult, OP.add)
-        t_chi = vec("ts", [b8], col(10), T.k8[:, :], (255 - hi_v) / 8.0, float(hi_v), OP.mult, OP.add)
-    padcol = {1: 5, 2: 6, 4: 7, 8: 8}
 
     own = slice(2 * 64, 3 * 64)
-    need("ve", [("ldx", 16)])
-    x1 = vec("tt", [t_x], T.xs[64:128, :], T.vraw[64:128, :], T.xio[64:128, :], OP.add)
-    need("ve", [("ldy", 16)])
-    ty = vec("ts", [t_row], T.vland[0:64, own], T.vraw[0:64, :], T.cols[0:64, 0:1], None, OP.add)
-    x2 = vec("ts", [x1], T.xm[64:128, :], T.xs[64:128, :], 63, None, OP.bitwise_and)
-    tx = vec("tc", [x2], T.vland[64:128, own], T.xm[64:128, :])
-
-    near = [t for t in range(n) if t != r and abs(t - r) <= 2]
+    c_0, c_63 = T.vland[64:128, 2 * 64:2 * 64 + 1], T.vland[64:128, 3 * 64 - 1:3 * 64]
+    need("ve", [("ldx", 16), ("ldy", 16)])
+    ta = vec("tt", [t_x, t_r], T.vland[:, own], T.vraw[:, :], T.ioc[:, :], OP.add)
+    t0 = vec("ts", [ta], c_0, c_0, -63.0, c_0, OP.mult, OP.max)
+    t63 = vec("ts", [], c_63, c_63, 64.0, c_63, OP.is_lt, OP.mult)
+    A0 = [ta, t0, t63]
 
     def same(t):
         return topo.chip(cores[t]) == topo.chip(core)
-    off, on = [t for t in near if not same(t)], [t for t in near if same(t)]
+    near = [t for t in range(n) if t != r and abs(t - r) <= 2]
+    off, on = outside(T, topo, r), [t for t in near if same(t)]
     mate = on[0]
-    far = [t for t in near if abs(t - r) == 2]
+    far = sorted([t for t in near if abs(t - r) == 2], key=lambda t: (t > r) == (mate > r))
     e_off = topo.engines(core, cores[off[0]])
     e_all = [e for e in topo.engines(core, cores[mate]) if e not in e_off]
     e_on = e_all[:4]
@@ -146,19 +167,43 @@ def rank_program(g, core, T, topo):
     def sname(kind, sender):
         return "%s%d" % (kind, sender % 5)
 
-    def transfer(buf, width, kind, sender, targets, engines):
+    def transfer(buf, width, lo, hi, kind, sender, targets, engines):
         k = sender - r + 2
-        ids = []
-        for t in targets:
-            rid, pid, _ = topo.addr(cores[t])
-            ids.append(DstId(rid=rid, pnc=pid))
-        return RemoteDMATransfer(dst_ids=ids, dma_engine_mask=bits(engines), remote_sem=S[sname(kind, sender)],
-                                 srcs=[buf[:, k * width:(k + 1) * width]],
-                                 dsts=[buf[:, (sender - t + 2) * width:(sender - t + 3) * width] for t in targets])
+        return RemoteDMATransfer(dst_ids=[address(topo, cores[t]) for t in targets], dma_engine_mask=bits(engines),
+                                 remote_sem=S[sname(kind, sender)], srcs=[buf[:, k * width + lo:k * width + hi]],
+                                 dsts=[buf[:, (sender - t + 2) * width + lo:(sender - t + 2) * width + hi]
+                                       for t in targets])
 
-    need("gp", [ty, tx])
-    g.remote_dma_fused([transfer(T.vland, 64, "va", r, on, e_on), transfer(T.vland, 64, "va", r, off, e_off)],
+    need("gp", A0)
+    g.remote_dma_fused([transfer(T.vland, 64, 0, 64, "va", r, on, e_on), transfer(T.vland, 64, 0, 64, "va", r, off, e_off)],
                        local_sem=S.lv)
+    part = 1024 - HELP
+    e_help, e_part = e_all[:HELP_ENGINES], e_all[HELP_ENGINES:]
+    g.wait_ge(S.ldi, 16)
+    g.remote_dma_fused([RemoteDMATransfer(dst_ids=[address(topo, helper(T, topo, r))], dma_engine_mask=bits(e_help),
+                                          remote_sem=S.hi, srcs=[T.pic[:, 2 * 1024 + part:3 * 1024]], dsts=[T.part[:, :]]),
+                        transfer(T.pic, 1024, part, 1024, "h", r, [mate], e_part)], local_sem=S.lh)
+    g.remote_dma_fused([transfer(T.pic, 1024, 0, part, "ia", r, far, e_off),
+                        transfer(T.pic, 1024, 0, part, "ia", r, [mate], e_all)], local_sem=S.li)
+    passed = r + 2 if mate > r else r - 2
+    n_f = 0
+    if 0 <= passed < n:
+        g.wait_ge(S[sname("ia", passed)], len(e_off))
+        g.remote_dma_fused([transfer(T.pic, 1024, 0, part, "ia", passed, [mate], e_all)], local_sem=S.lf)
+        n_f = len(e_all)
+
+    t_q = vec("ts", [t_q], T.qio[:, 8:128:16], T.qio[:, 8:128:16], -64.0, None, OP.add)
+    t_w = vec("ts", [t_15], col(12), c, 8.0, 8.0, OP.is_lt, OP.mult)
+    t_d = vec("ts", [], col(2), c, 9.0, float(base), OP.is_lt, OP.mult)
+    t_w = vec("ts", [t_w], col(3), c, 15.0, col(12), OP.is_ge, OP.add)
+    t_L = [vec("ts", [t_q, t_kf], T.lx[:, i * 128:(i + 1) * 128], T.qio[:, :], float(i), col(1), OP.add, OP.is_equal)
+           for i in range(8)]
+    t_z = vec("ts", [t_zi, t_16, t_w], T.z[:, :], T.zio[:, :], col(4), col(3), OP.is_equal, OP.mult)
+    t_pad = {}
+    padcol = {1: 5, 2: 6, 4: 7, 8: 8}
+    if edge is not None:
+        for k in (1, 2, 4, 8):
+            t_pad[k] = vec("ts", [], col(padcol[k]), c, 9.0, float(side * k), OP.is_lt, OP.mult)
 
     T0 = T.f0
     slots = [k for k in range(5) if 0 <= r + k - 2 < n]
@@ -169,13 +214,15 @@ def rank_program(g, core, T, topo):
         end0 = wh + 2
     ps_free = {}
     turn = [0]
+    spreads = {}
 
     def spread(k):
         if k == 2:
-            need("pe", t_L + [ty, tx])
+            need("pe", t_L + A0)
         else:
             t = r + k - 2
             need("pe", [(sname("va", t), len(e_on) if same(t) else len(e_off))])
+        spreads[k] = []
         for h in range(2):
             bank = (2 * turn[0] + h) % 8
             need("pe", ps_free.get(bank, []))
@@ -183,6 +230,11 @@ def rank_program(g, core, T, topo):
                 i = 4 * h + j
                 t = mark("pe", g.tensor.matmul(T.ps[:, bank * 512 + j * 64:bank * 512 + j * 64 + 64],
                                                T.lx[:, i * 128:(i + 1) * 128], T.vland[:, k * 64:k * 64 + 64], True, True))
+            spreads[k].append((bank, t))
+        turn[0] += 1
+
+    def settle(k):
+        for h, (bank, t) in enumerate(spreads[k]):
             out, src = T0[:, k * 512 + h * 256:k * 512 + h * 256 + 256], T.ps[:, bank * 512:bank * 512 + 256]
             if h == 0:
                 v = vec("ts", [t, t_d], out, src, col(2), None, OP.add)
@@ -190,7 +242,8 @@ def rank_program(g, core, T, topo):
                 v = act([t, t_d], out, src, IDENT, bias=col(2))
             wrote[0].append((8 * k + 4 * h, 8 * k + 4 * h + 4, v))
             ps_free[bank] = [v]
-        turn[0] += 1
+        if edge is not None and edge // 8 == k:
+            pads(0, 1)
 
     def pads(s, want):
         have = 1
@@ -213,90 +266,98 @@ def rank_program(g, core, T, topo):
                                            tabs[s][:, a * 64 + k:b * 64:16], k == 0, k == 15))
         return t
 
-    def note(s, a, b, bank, t, wbase):
-        v = vec("ts", [t], lists[s][:, a * 4:b * 4], T.ps[:, bank * 512:bank * 512 + (b - a) * 4], float(-64 * wbase),
-                None, OP.add)
+    def note(s, a, b, bank, t, wbase, skip=0):
+        v = vec("ts", [t], lists[s][:, a * 4:b * 4], T.ps[:, bank * 512 + skip * 4:bank * 512 + (skip + b - a) * 4],
+                float(-64 * wbase), None, OP.add)
         listed[s].append((a, b, v))
         ps_free[bank] = [v]
 
     def look(q, s, a, b, win):
         if a >= b:
             return
-        o = 16 if s == 3 else 0
         src = tabs[s][:, win[0] * 64:win[1] * 64].indirect(lists[s][:, a * 4:b * 4])
-        out = tabs[s + 1][:, (a - o) * 64:(b - o) * 64]
+        out = tabs[s + 1][:, a * 64:b * 64]
         deps = toks(wrote[s], win[0], win[1]) + toks(listed[s], a, b)
-        if q == "ve":
-            if s == 3 and edge is not None:
-                v = vec("ts", deps + [t_clo, t_chi], out, src, col(9), col(10), OP.max, OP.min)
-            else:
-                v = vec("tc", deps, out, src)
-        else:
-            v = act(deps, out, src, COPY)
-            if s == 3 and edge is not None:
-                v = vec("ts", [v, t_clo, t_chi], out, out, col(9), col(10), OP.max, OP.min)
+        v = vec("tc", deps, out, src) if q == "ve" else act(deps, out, src, COPY)
         wrote[s + 1].append((a, b, v))
 
-    def both(s, a, b, win):
+    def both(s, a, b, win, more=0):
         if a >= b:
             return
-        m = (a + b) // 2
-        if edge is not None and edge >= m:
-            look("ac", s, a, m, win)
-            look("ve", s, m, b, win)
+        m = (b - a) // 2 - more
+        if edge is not None and edge >= b - m:
+            look("ac", s, a, b - m, win)
+            look("ve", s, b - m, b, win)
         else:
-            look("ac", s, m, b, win)
-            look("ve", s, a, m, win)
+            look("ac", s, a + m, b, win)
+            look("ve", s, a, a + m, win)
 
     def real(a, b):
         return max(a, wl if wl is not None else a), min(b, wh + 1 if wh is not None else b)
 
     spread(2)
+    settle(2)
     tp = pick(0, 16, 24, 6)
-    tl = vec("ts", [tp], T.lland[:, 64:96], T.ps[:, 6 * 512:6 * 512 + 32], float(64 * (1 - base)), None, OP.add)
-    need("gp", [tl])
-    g.remote_dma_fused([transfer(T.lland, 32, "la", r, on, e_on), transfer(T.lland, 32, "la", r, off, e_off)],
-                       local_sem=S.ll)
-    g.wait_ge(S.ldi, 16)
-    g.remote_dma_fused([transfer(T.pic, 1024, "ia", r, far, e_off), transfer(T.pic, 1024, "ia", r, [mate], e_all)],
-                       local_sem=S.li)
-    passed = r + 2 if mate > r else r - 2
-    n_f = 0
-    if 0 <= passed < n:
-        g.wait_ge(S[sname("ia", passed)], len(e_off))
-        rid, pid, _ = topo.addr(cores[mate])
-        k = passed - r + 2
-        g.remote_dma(T.pic[:, (passed - mate + 2) * 1024:(passed - mate + 3) * 1024], T.pic[:, k * 1024:(k + 1) * 1024],
-                     S[sname("ia", passed)], S.lf, pid, rid, bits(e_all))
-        n_f = len(e_all)
 
-    if edge in (16, 23):
-        pads(0, 1)
+    d0, d1 = 2 * slots[0] + 1, 2 * slots[-1]
+    y1 = vec("ts", [t_1], col(13), T.k1[:, :], 1024.0, -512.0, OP.mult, OP.add)
+    x1 = vec("ts", [], col(14), c, -4.0, None, OP.mult)
+    y4 = vec("ts", [], col(15), c, 1.0, 64.0, OP.is_lt, OP.mult)
+    y2 = vec("ts", [y1], col(16), c, float(d0), col(13), OP.is_ge, OP.mult)
+    x2 = vec("ts", [x1], col(17), T.k1[:, :], -3.0, col(14), OP.mult, OP.add)
+    y5 = vec("ts", [y4], col(18), c, 15.0, col(15), OP.is_ge, OP.add)
+
     wide0 = {"own": (max(8, first0), min(32, end0)), "low": (first0, 24), "high": (16, end0)}
-    note(0, 16, 24, 6, tp, wide0["own"][0])
+    e0, e1 = (16 if wl == 16 else 17), (24 if wh == 23 else 23)
+    early = (15 if wl == 16 else 16, 25 if wh == 23 else 24)
+    note(0, e0, e1, 6, tp, early[0], e0 - 16)
+    both(0, e0, e1, early)
+    if e0 == 17:
+        note(0, 16, 17, 6, tp, wide0["own"][0])
+    if e1 == 23:
+        note(0, 23, 24, 6, tp, wide0["own"][0], 7)
+
+    y3 = vec("ts", [y2], col(19), c, float(d1), col(16), OP.is_le, OP.mult)
+    t_b = vec("ts", [x2], col(9), c, 9.0, col(17), OP.is_lt, OP.mult)
+    if wl is not None:
+        x3 = vec("ts", [], col(20), c, 1.0, float(-wl), OP.is_lt, OP.mult)
+        t_b = vec("tt", [t_b, x3], col(9), col(9), col(20), OP.add)
+    if wh is not None:
+        x3 = vec("ts", [], col(20), c, 8.0, float(32 - wh), OP.is_equal, OP.mult)
+        y6 = vec("ts", [], col(21), c, 8.0, -64.0, OP.is_equal, OP.mult)
+        t_b = vec("tt", [t_b, x3], col(9), col(9), col(20), OP.add)
+        y5 = vec("tt", [y5, y6], col(18), col(18), col(21), OP.add)
+    t_w4 = vec("tt", [y3, y5], col(10), col(19), col(18), OP.add)
+    t_z4 = vec("ts", [t_zi, t_16, t_w4], T.z4[:, :], T.zio[:, :], col(4), col(10), OP.is_equal, OP.mult)
+
+    order = sorted([k for k in (1, 3) if k in slots], key=lambda k: not same(r + k - 2))
+    outer = [k for k in ((0, 4) if 2 * r < n else (4, 0)) if k in slots]
     lowrows, highrows = real(2, 16), real(24, 38)
-
-    def fetch(k, a, b, wbase):
-        t = r + k - 2
-        need("ve", [(sname("la", t), len(e_on) if same(t) else len(e_off))])
-        v = vec("ts", [], lists[0][:, a * 4:b * 4], T.lland[:, 32 * k + (a - 8 * k) * 4:32 * k + (b - 8 * k) * 4],
-                float(-64 * (1 - base) - 64 * wbase), None, OP.add)
-        listed[0].append((a, b, v))
-
-    for k in sorted([k for k in (1, 3) if k in slots], key=lambda k: not same(r + k - 2)):
+    sides = [(k, rows, name) for k, rows, name in ((0, lowrows, "low"), (4, highrows, "high")) if rows[0] < rows[1]]
+    sides.sort(key=lambda x: outer.index(x[0]) + 1 if x[0] in outer else 0)
+    banks, tps = {0: 2, 4: 4}, {}
+    for k in order + outer[:1]:
         spread(k)
-        if edge in (8, 31) and edge // 8 == k:
-            pads(0, 1)
-    both(0, 16, 24, wide0["own"])
-    for k, rows, name in ((0, lowrows, "low"), (4, highrows, "high")):
-        if rows[0] >= rows[1]:
-            continue
-        if k in slots:
-            spread(k)
-        for q in (1, 0) if k == 0 else (3, 4):
-            if q in slots:
-                fetch(q, max(rows[0], 8 * q), min(rows[1], 8 * q + 8), wide0[name][0])
-        both(0, rows[0], rows[1], wide0[name])
+    for k in order:
+        settle(k)
+    if e0 == 17:
+        look("ve", 0, 16, 17, wide0["own"])
+    if e1 == 23:
+        look("ac", 0, 23, 24, wide0["own"])
+    for k in outer[:1]:
+        settle(k)
+    for k in outer[1:]:
+        spread(k)
+    for k, rows, name in sides:
+        if k not in outer[1:]:
+            tps[k] = pick(0, rows[0], rows[1], banks[k])
+    for k in outer[1:]:
+        settle(k)
+    for j, (k, rows, name) in enumerate(sides):
+        if k not in tps:
+            tps[k] = pick(0, rows[0], rows[1], banks[k])
+        note(0, rows[0], rows[1], banks[k], tps[k], wide0[name][0])
+        both(0, rows[0], rows[1], wide0[name], 1 - j)
 
     def window(lo, hi, reach):
         a, b = real(lo, hi)
@@ -314,56 +375,58 @@ def rank_program(g, core, T, topo):
         if wh is not None and win[1] > wh + 1:
             pads(s, win[1] - wh - 1)
 
-    a, b = real(4, 24)
+    low_first = sides[0][0] == 0
+    (a, b), (u, v) = [real(4, 24), real(24, 36)] if low_first else [real(16, 36), real(4, 16)]
     tp = pick(1, a, b, 0)
     finish(1, w1)
     note(1, a, b, 0, tp, w1[0])
-    c, d = real(24, 36)
-    if c < d:
-        tp2 = pick(1, c, d, 1)
-    both(1, a, b, w1)
-    if c < d:
-        note(1, c, d, 1, tp2, w1[0])
-        both(1, c, d, w1)
-    a, b = real(8, 24)
+    if u < v:
+        tp2 = pick(1, u, v, 1)
+    both(1, a, b, w1, 1)
+    if u < v:
+        note(1, u, v, 1, tp2, w1[0])
+        both(1, u, v, w1)
+    (a, b), (u, v) = [real(8, 24), real(24, 32)] if low_first else [real(16, 32), real(8, 16)]
     tp = pick(2, a, b, 2)
     finish(2, w2)
     note(2, a, b, 2, tp, w2[0])
-    c, d = real(24, 32)
-    if c < d:
-        tp2 = pick(2, c, d, 3)
+    if u < v:
+        tp2 = pick(2, u, v, 3)
     both(2, 16, 24, w2)
     tp3 = pick(3, 16, 24, 4)
-    both(2, a, min(b, 16), w2)
-    if c < d:
-        note(2, c, d, 3, tp2, w2[0])
-        both(2, c, d, w2)
+    if a < 16:
+        both(2, a, 16, w2)
+    else:
+        both(2, 24, b, w2)
+    if u < v:
+        note(2, u, v, 3, tp2, w2[0])
+        both(2, u, v, w2)
     finish(3, w3)
     note(3, 16, 24, 4, tp3, w3[0])
-    both(3, 16, 24, w3)
+    deps = toks(wrote[3], w3[0], w3[1]) + toks(listed[3], 16, 24) + [t_b]
+    src = T.f3[:, w3[0] * 64:w3[1] * 64]
+    v2 = act(deps, T.f4[:, 256:512], src.indirect(T.l3[:, 80:96]), RELU, bias=col(9))
+    v1 = vec("ts", deps, T.f4[:, 0:256], src.indirect(T.l3[:, 64:80]), col(9), 0.0, OP.add, OP.max)
 
-    need("pe", toks(wrote[4], 16, 24) + ps_free.get(5, []))
+    need("pe", [v1, v2] + ps_free.get(5, []) + [t_z4])
     for k in range(16):
-        tp = mark("pe", g.tensor.matmul(T.ps[:, 5 * 512:5 * 512 + 32], T.z[:, 15 - k:143 - k], T.f4[:, k:512:16],
+        tp = mark("pe", g.tensor.matmul(T.ps[:, 5 * 512:5 * 512 + 32], T.z4[:, 15 - k:143 - k], T.f4[:, k:512:16],
                                         k == 0, k == 15))
-    v = vec("tc", [tp], T.ca[:, :], T.ps[:, 5 * 512:5 * 512 + 32])
-    v = vec("ts", [v], T.cb[:, :], T.ca[:, :], 0xE00, None, OP.bitwise_and)
-    v = vec("tt", [v], T.cc[:, :], T.ca[:, :], T.cb[:, :], OP.add)
-    v = vec("ts", [v], T.l4[:, :], T.cc[:, :], float(-1024 * slots[0]), None, OP.add)
+    t4 = vec("tc", [tp], T.l4[:, :], T.ps[:, 5 * 512:5 * 512 + 32])
     arrived = [(sname("ia", t), len(e_off) if t in far else len(e_all)) for t in near] + [("ldi", 16)]
-    c0, c1 = slots[0] * 1024, slots[-1] * 1024 + 1024
+    arrived += [(sname("h", t), len(e_off) if t in off else len(e_part)) for t in near]
+    p0, p1 = slots[0] * 1024, slots[-1] * 1024 + 1024
     need("ve", arrived)
     need("ac", arrived)
-    va = vec("tc", [v], T.yo[:, 0:512], T.pic[:, c0:c1 - 512].indirect(T.l4[:, :]))
-    vb = act([v], T.yo[:, 512:1024], T.pic[:, c0 + 512:c1].indirect(T.l4[:, :]), COPY)
-    need("sy", [va])
-    g.sync.dma_start(T.y[:, 0:512], T.yo[:, 0:512]).then_inc(S.sta, 16)
-    need("ac", [vb])
-    g.scalar.dma_start(T.y[:, 512:1024], T.yo[:, 512:1024]).then_inc(S.stb, 16)
-    g.sync.wait_ge(S.sta, 16)
-    g.scalar.wait_ge(S.stb, 16)
+    for h in range(2):
+        a, src = 512 * h, T.pic[:, p0 + 512 * h:p1 - 512 + 512 * h]
+        v1 = vec("tc", [t4], T.yo[:, a:a + 256], src.indirect(T.l4[:, 0:16]))
+        v2 = act([t4], T.yo[:, a + 256:a + 512], src.indirect(T.l4[:, 16:32]), COPY)
+        need("sy", [v1, v2])
+        g.sync.dma_start(T.y[:, a:a + 512], T.yo[:, a:a + 512]).then_inc(S.sta, 16)
+    g.sync.wait_ge(S.sta, 32)
     g.wait_ge(S.lv, len(e_off) + len(e_on))
-    g.wait_ge(S.ll, len(e_off) + len(e_on))
+    g.wait_ge(S.lh, len(e_help) + len(e_part))
     g.wait_ge(S.li, len(e_off) + len(e_all))
     if n_f:
         g.wait_ge(S.lf, n_f)

@@ -34,10 +34,10 @@ SCRATCH = {
     "yo": ("sbuf", [128, 1024], "bfloat16"),
     "ps": ("psum", [128, 8 * 512], "float32"),
 }
-SEMAPHORES = (["ve", "ac", "pe", "gp", "ldy", "ldx", "ldi", "sta", "lv", "li", "lf", "lh", "hi", "hl"]
+SEMAPHORES = (["ve", "ac", "pe", "gp", "ldy", "ldx", "ldi", "sta", "lv", "li", "hi", "hl", "s0", "s1", "s2", "s3"]
               + [k + str(j) for k in ("va", "ia", "h") for j in range(5)])
 OP = AluOpType
-COPY, IDENT, RELU = ActivationFunctionType.Copy, ActivationFunctionType.Identity, ActivationFunctionType.Relu
+COPY, RELU = ActivationFunctionType.Copy, ActivationFunctionType.Relu
 
 
 def bits(engines):
@@ -53,6 +53,10 @@ def outside(T, topo, r):
     n = len(T.cores)
     there = [t for t in range(n) if abs(t - r) <= 2 and topo.chip(T.cores[t]) != topo.chip(T.cores[r])]
     return sorted(there, key=lambda t: (abs(t - r), min(t, n - 1 - t)))
+
+
+def other(T, topo, r):
+    return [t for t in range(len(T.cores)) if t != r and topo.chip(T.cores[t]) == topo.chip(T.cores[r])][0]
 
 
 def helper(T, topo, r):
@@ -154,15 +158,18 @@ def rank_program(g, core, T, topo):
     t63 = vec("ts", [], c_63, c_63, 64.0, c_63, OP.is_lt, OP.mult)
     A0 = [ta, t0, t63]
 
-    def same(t):
-        return topo.chip(cores[t]) == topo.chip(core)
     near = [t for t in range(n) if t != r and abs(t - r) <= 2]
-    off, on = outside(T, topo, r), [t for t in near if same(t)]
-    mate = on[0]
-    far = sorted([t for t in near if abs(t - r) == 2], key=lambda t: (t > r) == (mate > r))
+    off, mate = outside(T, topo, r), other(T, topo, r)
+    above = mate > r
+
+    def flip(a, b):
+        return (a, b) if above else (ROWS - b, ROWS - a)
+    k_near, k_far = (1, 0) if above else (3, 4)
+    outer = 0 <= r + k_near - 2 < n
+    fed = [t for t in off if (t > r) == (other(T, topo, t) > t)]
+    far = sorted([t for t in near if abs(t - r) == 2], key=lambda t: (t > r) == above)
     e_off = topo.engines(core, cores[off[0]])
     e_all = [e for e in topo.engines(core, cores[mate]) if e not in e_off]
-    e_on = e_all[:4]
 
     def sname(kind, sender):
         return "%s%d" % (kind, sender % 5)
@@ -173,55 +180,46 @@ def rank_program(g, core, T, topo):
                                  remote_sem=S[sname(kind, sender)], srcs=[buf[:, k * width + lo:k * width + hi]],
                                  dsts=[buf[:, (sender - t + 2) * width + lo:(sender - t + 2) * width + hi]
                                        for t in targets])
+    n_v = [0]
+
+    def share(s, rows, sem, engines):
+        a, b = rows
+        d = -8 if above else 8
+        need("gp", toks(wrote[s], a, b))
+        g.remote_dma_fused([RemoteDMATransfer(
+            dst_ids=[address(topo, cores[mate])], dma_engine_mask=bits(engines), remote_sem=S[sem],
+            srcs=[tabs[s][:, a * 64:b * 64]], dsts=[tabs[s][:, (a + d) * 64:(b + d) * 64]])], local_sem=S.lv)
+        n_v[0] += len(engines)
+
+    def take(s, rows, sem, engines):
+        a, b = rows
+        wrote[s].append(flip(48 - b, 48 - a) + ((sem, len(engines)),))
 
     need("gp", A0)
-    g.remote_dma_fused([transfer(T.vland, 64, 0, 64, "va", r, on, e_on), transfer(T.vland, 64, 0, 64, "va", r, off, e_off)],
-                       local_sem=S.lv)
+    g.remote_dma_fused([transfer(T.vland, 64, 0, 64, "va", r, fed, e_off)], local_sem=S.lv)
+    n_v[0] += len(e_off)
     part = 1024 - HELP
-    e_help, e_part = e_all[:HELP_ENGINES], e_all[HELP_ENGINES:]
+    e_help = e_all[:HELP_ENGINES]
     g.wait_ge(S.ldi, 16)
     g.remote_dma_fused([RemoteDMATransfer(dst_ids=[address(topo, helper(T, topo, r))], dma_engine_mask=bits(e_help),
-                                          remote_sem=S.hi, srcs=[T.pic[:, 2 * 1024 + part:3 * 1024]], dsts=[T.part[:, :]]),
-                        transfer(T.pic, 1024, part, 1024, "h", r, [mate], e_part)], local_sem=S.lh)
-    g.remote_dma_fused([transfer(T.pic, 1024, 0, part, "ia", r, far, e_off),
-                        transfer(T.pic, 1024, 0, part, "ia", r, [mate], e_all)], local_sem=S.li)
-    passed = r + 2 if mate > r else r - 2
-    n_f = 0
-    if 0 <= passed < n:
-        g.wait_ge(S[sname("ia", passed)], len(e_off))
-        g.remote_dma_fused([transfer(T.pic, 1024, 0, part, "ia", passed, [mate], e_all)], local_sem=S.lf)
-        n_f = len(e_all)
+                                          remote_sem=S.hi, srcs=[T.pic[:, 2 * 1024 + part:3 * 1024]],
+                                          dsts=[T.part[:, :]])], local_sem=S.li)
+    n_i = len(e_help)
 
     t_q = vec("ts", [t_q], T.qio[:, 8:128:16], T.qio[:, 8:128:16], -64.0, None, OP.add)
     t_w = vec("ts", [t_15], col(12), c, 8.0, 8.0, OP.is_lt, OP.mult)
-    t_d = vec("ts", [], col(2), c, 9.0, float(base), OP.is_lt, OP.mult)
-    t_w = vec("ts", [t_w], col(3), c, 15.0, col(12), OP.is_ge, OP.add)
     t_L = [vec("ts", [t_q, t_kf], T.lx[:, i * 128:(i + 1) * 128], T.qio[:, :], float(i), col(1), OP.add, OP.is_equal)
            for i in range(8)]
-    t_z = vec("ts", [t_zi, t_16, t_w], T.z[:, :], T.zio[:, :], col(4), col(3), OP.is_equal, OP.mult)
+
+    slots = [k for k in range(5) if 0 <= r + k - 2 < n]
     t_pad = {}
     padcol = {1: 5, 2: 6, 4: 7, 8: 8}
-    if edge is not None:
-        for k in (1, 2, 4, 8):
-            t_pad[k] = vec("ts", [], col(padcol[k]), c, 9.0, float(side * k), OP.is_lt, OP.mult)
-
-    T0 = T.f0
-    slots = [k for k in range(5) if 0 <= r + k - 2 < n]
-    first0, end0 = 8 * slots[0], 8 * slots[-1] + 8
-    if wl is not None:
-        first0 = wl - 1
-    if wh is not None:
-        end0 = wh + 2
     ps_free = {}
     turn = [0]
     spreads = {}
 
     def spread(k):
-        if k == 2:
-            need("pe", t_L + A0)
-        else:
-            t = r + k - 2
-            need("pe", [(sname("va", t), len(e_on) if same(t) else len(e_off))])
+        need("pe", t_L + (A0 if k == 2 else [(sname("va", r + k - 2), len(e_off))]))
         spreads[k] = []
         for h in range(2):
             bank = (2 * turn[0] + h) % 8
@@ -235,15 +233,10 @@ def rank_program(g, core, T, topo):
 
     def settle(k):
         for h, (bank, t) in enumerate(spreads[k]):
-            out, src = T0[:, k * 512 + h * 256:k * 512 + h * 256 + 256], T.ps[:, bank * 512:bank * 512 + 256]
-            if h == 0:
-                v = vec("ts", [t, t_d], out, src, col(2), None, OP.add)
-            else:
-                v = act([t, t_d], out, src, IDENT, bias=col(2))
+            out, src = T.f0[:, k * 512 + h * 256:k * 512 + h * 256 + 256], T.ps[:, bank * 512:bank * 512 + 256]
+            v = vec("tc", [t], out, src) if h == 0 else act([t], out, src, COPY)
             wrote[0].append((8 * k + 4 * h, 8 * k + 4 * h + 4, v))
             ps_free[bank] = [v]
-        if edge is not None and edge // 8 == k:
-            pads(0, 1)
 
     def pads(s, want):
         have = 1
@@ -258,17 +251,20 @@ def rank_program(g, core, T, topo):
             wrote[s].append((d0, d0 + m, v))
             have += m
 
-    def pick(s, a, b, bank):
+    def pick(s, rows, bank):
+        a, b = rows
         cells = (b - a) * 64
         need("pe", toks(wrote[s], a, b) + ps_free.get(bank, []) + [t_z])
         for k in range(16):
             t = mark("pe", g.tensor.matmul(T.ps[:, bank * 512:bank * 512 + cells // 16], T.z[:, 15 - k:143 - k],
                                            tabs[s][:, a * 64 + k:b * 64:16], k == 0, k == 15))
-        return t
+        return a, bank, t
 
-    def note(s, a, b, bank, t, wbase, skip=0):
-        v = vec("ts", [t], lists[s][:, a * 4:b * 4], T.ps[:, bank * 512 + skip * 4:bank * 512 + (skip + b - a) * 4],
-                float(-64 * wbase), None, OP.add)
+    def note(s, rows, got, win):
+        a, b = rows
+        top, bank, t = got
+        v = vec("ts", [t], lists[s][:, a * 4:b * 4], T.ps[:, bank * 512 + (a - top) * 4:bank * 512 + (b - top) * 4],
+                float(64 * (base - win[0])), None, OP.add)
         listed[s].append((a, b, v))
         ps_free[bank] = [v]
 
@@ -281,10 +277,11 @@ def rank_program(g, core, T, topo):
         v = vec("tc", deps, out, src) if q == "ve" else act(deps, out, src, COPY)
         wrote[s + 1].append((a, b, v))
 
-    def both(s, a, b, win, more=0):
+    def both(s, rows, win):
+        a, b = rows
         if a >= b:
             return
-        m = (b - a) // 2 - more
+        m = (b - a) // 2
         if edge is not None and edge >= b - m:
             look("ac", s, a, b - m, win)
             look("ve", s, b - m, b, win)
@@ -292,30 +289,54 @@ def rank_program(g, core, T, topo):
             look("ac", s, a + m, b, win)
             look("ve", s, a, a + m, win)
 
-    def real(a, b):
+    def real(rows):
+        a, b = rows
         return max(a, wl if wl is not None else a), min(b, wh + 1 if wh is not None else b)
 
+    def window(rows, reach):
+        a, b = rows
+        return max(a, wl - reach if wl is not None else a), min(b, wh + 1 + reach if wh is not None else b)
+
+    def finish(s, win):
+        if wl is not None and win[0] < wl:
+            pads(s, wl - win[0])
+        if wh is not None and win[1] > wh + 1:
+            pads(s, win[1] - wh - 1)
+
     spread(2)
+    t_w = vec("ts", [t_w], col(3), c, 15.0, col(12), OP.is_ge, OP.add)
+    if edge is not None:
+        for k in (1, 2, 4, 8):
+            t_pad[k] = vec("ts", [t_15], col(padcol[k]), c, 9.0, float(side * k), OP.is_lt, OP.mult)
+    t_z = vec("ts", [t_zi, t_16, t_w], T.z[:, :], T.zio[:, :], col(4), col(3), OP.is_equal, OP.mult)
     settle(2)
-    tp = pick(0, 16, 24, 6)
+    if not outer:
+        pads(0, 1)
+    share(0, flip(23, 24), "s0", e_off)
+    take(0, (23, 24), "s0", e_off)
+    g.remote_dma_fused([transfer(T.pic, 1024, 0, part, "ia", r, far, e_off)], local_sem=S.li)
+    n_i += len(e_off)
+    got = pick(0, (16, 24), 6)
 
     d0, d1 = 2 * slots[0] + 1, 2 * slots[-1]
     y1 = vec("ts", [t_1], col(13), T.k1[:, :], 1024.0, -512.0, OP.mult, OP.add)
-    x1 = vec("ts", [], col(14), c, -4.0, None, OP.mult)
+    x1 = vec("ts", [], col(14), c, -4.0, float(base), OP.mult, OP.add)
     y4 = vec("ts", [], col(15), c, 1.0, 64.0, OP.is_lt, OP.mult)
     y2 = vec("ts", [y1], col(16), c, float(d0), col(13), OP.is_ge, OP.mult)
     x2 = vec("ts", [x1], col(17), T.k1[:, :], -3.0, col(14), OP.mult, OP.add)
     y5 = vec("ts", [y4], col(18), c, 15.0, col(15), OP.is_ge, OP.add)
 
-    wide0 = {"own": (max(8, first0), min(32, end0)), "low": (first0, 24), "high": (16, end0)}
-    e0, e1 = (16 if wl == 16 else 17), (24 if wh == 23 else 23)
-    early = (15 if wl == 16 else 16, 25 if wh == 23 else 24)
-    note(0, e0, e1, 6, tp, early[0], e0 - 16)
-    both(0, e0, e1, early)
-    if e0 == 17:
-        note(0, 16, 17, 6, tp, wide0["own"][0])
-    if e1 == 23:
-        note(0, 23, 24, 6, tp, wide0["own"][0], 7)
+    first = flip(17 if outer else 16, 23)
+    early = flip(16 if outer else 15, 24)
+    inner, nearwin, farwin = flip(16 if outer else 15, 25), flip(8, 24), flip(0, 16)
+    note(0, first, got, early)
+    both(0, first, early)
+    note(0, flip(23, 24), got, inner)
+    if outer:
+        note(0, flip(16, 17), got, nearwin)
+    look("ac", 0, *flip(23, 24), inner)
+    share(1, first, "s1", e_all)
+    share(1, flip(23, 24), "s2", e_all)
 
     y3 = vec("ts", [y2], col(19), c, float(d1), col(16), OP.is_le, OP.mult)
     t_b = vec("ts", [x2], col(9), c, 9.0, col(17), OP.is_lt, OP.mult)
@@ -330,81 +351,72 @@ def rank_program(g, core, T, topo):
     t_w4 = vec("tt", [y3, y5], col(10), col(19), col(18), OP.add)
     t_z4 = vec("ts", [t_zi, t_16, t_w4], T.z4[:, :], T.zio[:, :], col(4), col(10), OP.is_equal, OP.mult)
 
-    order = sorted([k for k in (1, 3) if k in slots], key=lambda k: not same(r + k - 2))
-    outer = [k for k in ((0, 4) if 2 * r < n else (4, 0)) if k in slots]
-    lowrows, highrows = real(2, 16), real(24, 38)
-    sides = [(k, rows, name) for k, rows, name in ((0, lowrows, "low"), (4, highrows, "high")) if rows[0] < rows[1]]
-    sides.sort(key=lambda x: outer.index(x[0]) + 1 if x[0] in outer else 0)
-    banks, tps = {0: 2, 4: 4}, {}
-    for k in order + outer[:1]:
-        spread(k)
-    for k in order:
-        settle(k)
-    if e0 == 17:
-        look("ve", 0, 16, 17, wide0["own"])
-    if e1 == 23:
-        look("ac", 0, 23, 24, wide0["own"])
-    for k in outer[:1]:
-        settle(k)
-    for k in outer[1:]:
-        spread(k)
-    for k, rows, name in sides:
-        if k not in outer[1:]:
-            tps[k] = pick(0, rows[0], rows[1], banks[k])
-    for k in outer[1:]:
-        settle(k)
-    for j, (k, rows, name) in enumerate(sides):
-        if k not in tps:
-            tps[k] = pick(0, rows[0], rows[1], banks[k])
-        note(0, rows[0], rows[1], banks[k], tps[k], wide0[name][0])
-        both(0, rows[0], rows[1], wide0[name], 1 - j)
+    if outer:
+        spread(k_near)
+        spread(k_far)
+        settle(k_near)
+        got = pick(0, flip(8, 16), 7)
+        settle(k_far)
+        got2 = pick(0, flip(2, 8), 6)
+        note(0, flip(9, 16), got, nearwin)
+        both(0, flip(9, 17), nearwin)
+        share(1, flip(10, 17), "s3", e_all)
+        note(0, flip(8, 9), got, farwin)
+    mates_outer = 0 <= (mate + 1 if above else mate - 1) < n
+    take(1, (17 if mates_outer else 16, 23), "s1", e_all)
+    take(1, (23, 24), "s2", e_all)
+    if mates_outer:
+        take(1, (10, 17), "s3", e_all)
 
-    def window(lo, hi, reach):
-        a, b = real(lo, hi)
-        if wl is not None:
-            a = max(lo, wl - reach)
-        if wh is not None:
-            b = min(hi, wh + 1 + reach)
-        return a, b
-
-    w1, w2, w3 = window(2, 38, 2), window(4, 36, 4), window(8, 32, 8)
-
-    def finish(s, win):
-        if wl is not None and win[0] < wl:
-            pads(s, wl - win[0])
-        if wh is not None and win[1] > wh + 1:
-            pads(s, win[1] - wh - 1)
-
-    low_first = sides[0][0] == 0
-    (a, b), (u, v) = [real(4, 24), real(24, 36)] if low_first else [real(16, 36), real(4, 16)]
-    tp = pick(1, a, b, 0)
-    finish(1, w1)
-    note(1, a, b, 0, tp, w1[0])
-    if u < v:
-        tp2 = pick(1, u, v, 1)
-    both(1, a, b, w1, 1)
-    if u < v:
-        note(1, u, v, 1, tp2, w1[0])
-        both(1, u, v, w1)
-    (a, b), (u, v) = [real(8, 24), real(24, 32)] if low_first else [real(16, 32), real(8, 16)]
-    tp = pick(2, a, b, 2)
-    finish(2, w2)
-    note(2, a, b, 2, tp, w2[0])
-    if u < v:
-        tp2 = pick(2, u, v, 3)
-    both(2, 16, 24, w2)
-    tp3 = pick(3, 16, 24, 4)
-    if a < 16:
-        both(2, a, 16, w2)
+    p1, p2, p3 = flip(12 if outer else 16, 28), flip(4, 12), real(flip(28, 36))
+    w1, w2, w3 = window(flip(10 if outer else 14, 30), 2), flip(2, 14), window(flip(26, 38), 2)
+    g1 = pick(1, p1, 0)
+    if outer:
+        note(0, flip(2, 8), got2, farwin)
+        both(0, flip(2, 9), farwin)
+        g2 = pick(1, p2, 1)
     else:
-        both(2, 24, b, w2)
-    if u < v:
-        note(2, u, v, 3, tp2, w2[0])
-        both(2, u, v, w2)
-    finish(3, w3)
-    note(3, 16, 24, 4, tp3, w3[0])
-    deps = toks(wrote[3], w3[0], w3[1]) + toks(listed[3], 16, 24) + [t_b]
-    src = T.f3[:, w3[0] * 64:w3[1] * 64]
+        finish(1, w1)
+    note(1, p1, g1, w1)
+    both(1, p1, w1)
+    if outer:
+        note(1, p2, g2, w2)
+        both(1, p2, w2)
+        finish(1, w3)
+    g.remote_dma_fused([transfer(T.pic, 1024, part, 1024, "h", r, [mate], e_all)], local_sem=S.li)
+    n_i += len(e_all)
+    passed = r + 2 if above else r - 2
+    inside = [transfer(T.pic, 1024, 0, part, "ia", r, [mate], e_all)]
+    n_i += len(e_all)
+    if 0 <= passed < n:
+        g.wait_ge(S[sname("ia", passed)], len(e_off))
+        inside.append(transfer(T.pic, 1024, 0, part, "ia", passed, [mate], e_off))
+        n_i += len(e_off)
+    g.remote_dma_fused(inside, local_sem=S.li)
+
+    x1 = window(flip(4 if outer else 12, 28), 4)
+    x2, x3 = window(flip(20, 36), 4), window((8, 32), 8)
+    q1, q2 = flip(8 if outer else 16, 24), real(flip(24, 32))
+    g3 = pick(1, p3, 2)
+    g4 = pick(2, q1, 3)
+    if not outer:
+        finish(2, x1)
+    note(1, p3, g3, w3)
+    both(1, p3, w3)
+    g5 = pick(2, q2, 4)
+    if outer:
+        finish(2, x2)
+    note(2, q1, g4, x1)
+    both(2, (16, 24), x1)
+    g6 = pick(3, (16, 24), 7)
+    if outer:
+        both(2, flip(8, 16), x1)
+    note(2, q2, g5, x2)
+    both(2, q2, x2)
+    finish(3, x3)
+    note(3, (16, 24), g6, x3)
+    deps = toks(wrote[3], x3[0], x3[1]) + toks(listed[3], 16, 24) + [t_b]
+    src = T.f3[:, x3[0] * 64:x3[1] * 64]
     v2 = act(deps, T.f4[:, 256:512], src.indirect(T.l3[:, 80:96]), RELU, bias=col(9))
     v1 = vec("ts", deps, T.f4[:, 0:256], src.indirect(T.l3[:, 64:80]), col(9), 0.0, OP.add, OP.max)
 
@@ -413,8 +425,8 @@ def rank_program(g, core, T, topo):
         tp = mark("pe", g.tensor.matmul(T.ps[:, 5 * 512:5 * 512 + 32], T.z4[:, 15 - k:143 - k], T.f4[:, k:512:16],
                                         k == 0, k == 15))
     t4 = vec("tc", [tp], T.l4[:, :], T.ps[:, 5 * 512:5 * 512 + 32])
-    arrived = [(sname("ia", t), len(e_off) if t in far else len(e_all)) for t in near] + [("ldi", 16)]
-    arrived += [(sname("h", t), len(e_off) if t in off else len(e_part)) for t in near]
+    arrived = [(sname("ia", t), len(e_all) if t == mate else len(e_off)) for t in near]
+    arrived += [(sname("h", t), len(e_all) if t == mate else len(e_off)) for t in near] + [("ldi", 16)]
     p0, p1 = slots[0] * 1024, slots[-1] * 1024 + 1024
     need("ve", arrived)
     need("ac", arrived)
@@ -425,11 +437,8 @@ def rank_program(g, core, T, topo):
         need("sy", [v1, v2])
         g.sync.dma_start(T.y[:, a:a + 512], T.yo[:, a:a + 512]).then_inc(S.sta, 16)
     g.sync.wait_ge(S.sta, 32)
-    g.wait_ge(S.lv, len(e_off) + len(e_on))
-    g.wait_ge(S.lh, len(e_help) + len(e_part))
-    g.wait_ge(S.li, len(e_off) + len(e_all))
-    if n_f:
-        g.wait_ge(S.lf, n_f)
+    g.wait_ge(S.lv, n_v[0])
+    g.wait_ge(S.li, n_i)
     for q in ("ve", "ac", "pe"):
         g.wait_ge(S[q], done[q])
     g.wait_ge(S.gp, done["gp"])

from concourse.bass import DstId, RemoteDMATransfer
from concourse.mybir import AluOpType, ActivationFunctionType

HELP = 320
HELP_ENGINES = 4
ROWS = 40
SCRATCH = {
    "vraw": ("sbuf", [128, 64], "int32"),
    "ioc": ("sbuf", [128, 64], "int32"),
    "vland": ("sbuf", [128, 5 * 64], "bfloat16"),
    "kidx": ("sbuf", [128, 1], "int32"),
    "k1": ("sbuf", [128, 1], "int32"),
    "k7": ("sbuf", [128, 1], "int32"),
    "k15": ("sbuf", [128, 1], "int32"),
    "k16": ("sbuf", [128, 1], "int32"),
    "cols": ("sbuf", [128, 32], "float32"),
    "qio": ("sbuf", [128, 128], "bfloat16"),
    "zio": ("sbuf", [128, 144], "bfloat16"),
    "lx": ("sbuf", [128, 8 * 128], "bfloat16"),
    "z": ("sbuf", [128, 144], "bfloat16"),
    "z4": ("sbuf", [128, 144], "bfloat16"),
    "f0": ("sbuf", [128, ROWS * 64], "bfloat16"),
    "f1": ("sbuf", [128, ROWS * 64], "bfloat16"),
    "f2": ("sbuf", [128, ROWS * 64], "bfloat16"),
    "f3": ("sbuf", [128, ROWS * 64], "bfloat16"),
    "f4": ("sbuf", [128, 512], "bfloat16"),
    "l0": ("sbuf", [128, ROWS * 4], "uint16"),
    "l1": ("sbuf", [128, ROWS * 4], "uint16"),
    "l2": ("sbuf", [128, ROWS * 4], "uint16"),
    "l3": ("sbuf", [128, ROWS * 4], "uint16"),
    "l4": ("sbuf", [128, 32], "uint16"),
    "pic": ("sbuf", [128, 5 * 1024], "bfloat16"),
    "part": ("sbuf", [128, HELP], "bfloat16"),
    "yo": ("sbuf", [128, 1024], "bfloat16"),
    "ps": ("psum", [128, 8 * 512], "float32"),
}
SEMAPHORES = (["ve", "ac", "pe", "gp", "ldy", "ldx", "ldi", "sta", "lv", "li", "hi", "hl", "s0", "s1", "s2", "s3"]
              + [k + str(j) for k in ("va", "ia", "h") for j in range(5)])
OP = AluOpType
COPY, RELU = ActivationFunctionType.Copy, ActivationFunctionType.Relu


def bits(engines):
    return sum(1 << e for e in engines)


def address(topo, c):
    rid, pid, _ = topo.addr(c)
    return DstId(rid=rid, pnc=pid)


def outside(T, topo, r):
    n = len(T.cores)
    there = [t for t in range(n) if abs(t - r) <= 2 and topo.chip(T.cores[t]) != topo.chip(T.cores[r])]
    return sorted(there, key=lambda t: (abs(t - r), min(t, n - 1 - t)))


def other(T, topo, r):
    return [t for t in range(len(T.cores)) if t != r and topo.chip(T.cores[t]) == topo.chip(T.cores[r])][0]


def helper(T, topo, r):
    me = T.cores[r]
    here = [c for c in T.cores if topo.chip(c) == topo.chip(me)]
    free = [c for c in topo.cores_of(me) if c not in T.cores and topo.die(c) != topo.die(me)
            and all(topo.may_write(c, T.cores[t]) for t in outside(T, topo, r))]
    return free[here.index(me)]


def relay(g, core, T, topo, r):
    off = outside(T, topo, r)
    es = topo.engines(core, T.cores[off[0]])
    g.wait_ge(T.sem.hi, HELP_ENGINES)
    g.remote_dma_fused([RemoteDMATransfer(
        dst_ids=[address(topo, T.cores[t]) for t in off], dma_engine_mask=bits(es), remote_sem=T.sem["h%d" % (r % 5)],
        srcs=[T.part[:, :]], dsts=[T.pic[:, (r - t + 3) * 1024 - HELP:(r - t + 3) * 1024] for t in off])],
        local_sem=T.sem.hl)
    g.wait_ge(T.sem.hl, len(es))


def rank_program(g, core, T, topo):
    r = T.rank_of(core)
    if r is None:
        for r in range(len(T.cores)):
            if helper(T, topo, r) == core:
                relay(g, core, T, topo, r)
        return
    cores = list(T.cores)
    n = len(cores)
    S = T.sem
    queues = {"ve": g.vector, "ac": g.scalar, "pe": g.tensor, "gp": g, "sy": g.sync}
    done = {"ve": 0, "ac": 0, "pe": 0, "gp": 0}
    seen = {q: {} for q in queues}

    def need(q, deps):
        best = {}
        for s, v in deps:
            best[s] = max(best.get(s, 0), v)
        for s, v in best.items():
            if seen[q].get(s, 0) < v:
                queues[q].wait_ge(S[s], v)
                seen[q][s] = v

    def mark(q, ins):
        ins.then_inc(S[q], 1)
        done[q] += 1
        return (q, done[q])

    def vec(name, deps, *args):
        need("ve", deps)
        f = {"ts": g.vector.tensor_scalar, "tt": g.vector.tensor_tensor, "tc": g.vector.tensor_copy}[name]
        return mark("ve", f(*args))

    def act(deps, out, in_, func, **kw):
        need("ac", deps)
        return mark("ac", g.scalar.activation(out, in_, func, **kw))

    tabs = [T.f0, T.f1, T.f2, T.f3, T.f4]
    lists = [T.l0, T.l1, T.l2, T.l3]
    wrote = [[], [], [], [], []]
    listed = [[], [], [], []]

    def toks(book, a, b):
        return [t for lo, hi, t in book if lo < b and a < hi]

    g.sync.dma_start(T.vraw[0:64, :], T.vy[:, :]).then_inc(S.ldy, 16)
    g.scalar.dma_start(T.vraw[64:128, :], T.vx[:, :]).then_inc(S.ldx, 16)
    g.sync.dma_start(T.pic[:, 2 * 1024:3 * 1024], T.img[:, :]).then_inc(S.ldi, 16)

    t_k = mark("gp", g.iota(T.kidx[:, :], [[1, 1]], 0, 1))
    t_x = mark("gp", g.iota(T.ioc[:, :], [[1, 64]], 0, 0))
    t_q = mark("gp", g.iota(T.qio[:, :], [[8, 8], [64, 2], [0, 8]], 0, 0, allow_small_or_imprecise_dtypes=True))
    t_zi = mark("gp", g.iota(T.zio[:, :], [[1, 144]], -15, 0, allow_small_or_imprecise_dtypes=True))

    def col(j):
        return T.cols[:, j:j + 1]
    c = col(11)
    k7 = vec("ts", [t_k], T.k7[:, :], T.kidx[:, :], 7, None, OP.bitwise_and)
    c15 = vec("ts", [], T.k15[:, :], T.kidx[:, :], 15, None, OP.bitwise_and)
    t_row = vec("ts", [k7], col(0), T.k7[:, :], float(8 * r), None, OP.add)
    c16 = vec("ts", [], T.k16[:, :], T.kidx[:, :], 112, None, OP.bitwise_and)
    t_r = vec("ts", [t_row, t_x], T.ioc[0:64, :], T.ioc[0:64, :], 0.0, T.cols[0:64, 0:1], OP.mult, OP.add)
    t_kf = vec("tc", [], col(1), T.kidx[:, :])
    t_15 = vec("tc", [c15], c, T.k15[:, :])
    t_16 = vec("tc", [c16], col(4), T.k16[:, :])
    t_1 = vec("ts", [], T.k1[:, :], T.kidx[:, :], 1, None, OP.bitwise_and)
    base = 16 - 8 * r
    wl = base if base > 0 else None
    wh = base + 8 * n - 1 if base + 8 * n - 1 < ROWS - 1 else None
    side = -1 if wl is not None else 1
    edge = wl if wl is not None else wh

    own = slice(2 * 64, 3 * 64)
    c_0, c_63 = T.vland[64:128, 2 * 64:2 * 64 + 1], T.vland[64:128, 3 * 64 - 1:3 * 64]
    need("ve", [("ldx", 16), ("ldy", 16)])
    ta = vec("tt", [t_x, t_r], T.vland[:, own], T.vraw[:, :], T.ioc[:, :], OP.add)
    t0 = vec("ts", [ta], c_0, c_0, -63.0, c_0, OP.mult, OP.max)
    t63 = vec("ts", [], c_63, c_63, 64.0, c_63, OP.is_lt, OP.mult)
    A0 = [ta, t0, t63]

    near = [t for t in range(n) if t != r and abs(t - r) <= 2]
    off, mate = outside(T, topo, r), other(T, topo, r)
    above = mate > r

    def flip(a, b):
        return (a, b) if above else (ROWS - b, ROWS - a)
    k_near, k_far = (1, 0) if above else (3, 4)
    outer = 0 <= r + k_near - 2 < n
    fed = [t for t in off if (t > r) == (other(T, topo, t) > t)]
    far = sorted([t for t in near if abs(t - r) == 2], key=lambda t: (t > r) == above)
    e_off = topo.engines(core, cores[off[0]])
    e_all = [e for e in topo.engines(core, cores[mate]) if e not in e_off]

    def sname(kind, sender):
        return "%s%d" % (kind, sender % 5)

    def transfer(buf, width, lo, hi, kind, sender, targets, engines):
        k = sender - r + 2
        return RemoteDMATransfer(dst_ids=[address(topo, cores[t]) for t in targets], dma_engine_mask=bits(engines),
                                 remote_sem=S[sname(kind, sender)], srcs=[buf[:, k * width + lo:k * width + hi]],
                                 dsts=[buf[:, (sender - t + 2) * width + lo:(sender - t + 2) * width + hi]
                                       for t in targets])
    n_v = [0]

    def share(s, rows, sem, engines):
        a, b = rows
        d = -8 if above else 8
        need("gp", toks(wrote[s], a, b))
        g.remote_dma_fused([RemoteDMATransfer(
            dst_ids=[address(topo, cores[mate])], dma_engine_mask=bits(engines), remote_sem=S[sem],
            srcs=[tabs[s][:, a * 64:b * 64]], dsts=[tabs[s][:, (a + d) * 64:(b + d) * 64]])], local_sem=S.lv)
        n_v[0] += len(engines)

    def take(s, rows, sem, engines):
        a, b = rows
        wrote[s].append(flip(48 - b, 48 - a) + ((sem, len(engines)),))

    need("gp", A0)
    g.remote_dma_fused([transfer(T.vland, 64, 0, 64, "va", r, fed, e_off)], local_sem=S.lv)
    n_v[0] += len(e_off)
    part = 1024 - HELP
    e_help = e_all[:HELP_ENGINES]
    g.wait_ge(S.ldi, 16)
    g.remote_dma_fused([RemoteDMATransfer(dst_ids=[address(topo, helper(T, topo, r))], dma_engine_mask=bits(e_help),
                                          remote_sem=S.hi, srcs=[T.pic[:, 2 * 1024 + part:3 * 1024]],
                                          dsts=[T.part[:, :]])], local_sem=S.li)
    n_i = len(e_help)

    t_q = vec("ts", [t_q], T.qio[:, 8:128:16], T.qio[:, 8:128:16], -64.0, None, OP.add)
    t_w = vec("ts", [t_15], col(12), c, 8.0, 8.0, OP.is_lt, OP.mult)
    t_L = [vec("ts", [t_q, t_kf], T.lx[:, i * 128:(i + 1) * 128], T.qio[:, :], float(i), col(1), OP.add, OP.is_equal)
           for i in range(8)]

    slots = [k for k in range(5) if 0 <= r + k - 2 < n]
    t_pad = {}
    padcol = {1: 5, 2: 6, 4: 7, 8: 8}
    ps_free = {}
    turn = [0]
    spreads = {}

    def spread(k):
        need("pe", t_L + (A0 if k == 2 else [(sname("va", r + k - 2), len(e_off))]))
        spreads[k] = []
        for h in range(2):
            bank = (2 * turn[0] + h) % 8
            need("pe", ps_free.get(bank, []))
            for j in range(4):
                i = 4 * h + j
                t = mark("pe", g.tensor.matmul(T.ps[:, bank * 512 + j * 64:bank * 512 + j * 64 + 64],
                                               T.lx[:, i * 128:(i + 1) * 128], T.vland[:, k * 64:k * 64 + 64], True, True))
            spreads[k].append((bank, t))
        turn[0] += 1

    def settle(k):
        for h, (bank, t) in enumerate(spreads[k]):
            out, src = T.f0[:, k * 512 + h * 256:k * 512 + h * 256 + 256], T.ps[:, bank * 512:bank * 512 + 256]
            v = vec("tc", [t], out, src) if h == 0 else act([t], out, src, COPY)
            wrote[0].append((8 * k + 4 * h, 8 * k + 4 * h + 4, v))
            ps_free[bank] = [v]

    def pads(s, want):
        have = 1
        while have <= want:
            m = min(have, want + 1 - have)
            if side < 0:
                d0, s0 = edge - have - m + 1, edge - m + 1
            else:
                d0, s0 = edge + have, edge
            v = vec("ts", toks(wrote[s], s0, s0 + m) + [t_pad[have]], tabs[s][:, d0 * 64:(d0 + m) * 64],
                    tabs[s][:, s0 * 64:(s0 + m) * 64], col(padcol[have]), None, OP.add)
            wrote[s].append((d0, d0 + m, v))
            have += m

    def pick(s, rows, bank):
        a, b = rows
        cells = (b - a) * 64
        need("pe", toks(wrote[s], a, b) + ps_free.get(bank, []) + [t_z])
        for k in range(16):
            t = mark("pe", g.tensor.matmul(T.ps[:, bank * 512:bank * 512 + cells // 16], T.z[:, 15 - k:143 - k],
                                           tabs[s][:, a * 64 + k:b * 64:16], k == 0, k == 15))
        return a, bank, t

    def note(s, rows, got, win):
        a, b = rows
        top, bank, t = got
        v = vec("ts", [t], lists[s][:, a * 4:b * 4], T.ps[:, bank * 512 + (a - top) * 4:bank * 512 + (b - top) * 4],
                float(64 * (base - win[0])), None, OP.add)
        listed[s].append((a, b, v))
        ps_free[bank] = [v]

    def look(q, s, a, b, win):
        if a >= b:
            return
        src = tabs[s][:, win[0] * 64:win[1] * 64].indirect(lists[s][:, a * 4:b * 4])
        out = tabs[s + 1][:, a * 64:b * 64]
        deps = toks(wrote[s], win[0], win[1]) + toks(listed[s], a, b)
        v = vec("tc", deps, out, src) if q == "ve" else act(deps, out, src, COPY)
        wrote[s + 1].append((a, b, v))

    def both(s, rows, win):
        a, b = rows
        if a >= b:
            return
        m = (b - a) // 2
        if edge is not None and edge >= b - m:
            look("ac", s, a, b - m, win)
            look("ve", s, b - m, b, win)
        else:
            look("ac", s, a + m, b, win)
            look("ve", s, a, a + m, win)

    def real(rows):
        a, b = rows
        return max(a, wl if wl is not None else a), min(b, wh + 1 if wh is not None else b)

    def window(rows, reach):
        a, b = rows
        return max(a, wl - reach if wl is not None else a), min(b, wh + 1 + reach if wh is not None else b)

    def finish(s, win):
        if wl is not None and win[0] < wl:
            pads(s, wl - win[0])
        if wh is not None and win[1] > wh + 1:
            pads(s, win[1] - wh - 1)

    spread(2)
    t_w = vec("ts", [t_w], col(3), c, 15.0, col(12), OP.is_ge, OP.add)
    if edge is not None:
        for k in (1, 2, 4, 8):
            t_pad[k] = vec("ts", [t_15], col(padcol[k]), c, 9.0, float(side * k), OP.is_lt, OP.mult)
    t_z = vec("ts", [t_zi, t_16, t_w], T.z[:, :], T.zio[:, :], col(4), col(3), OP.is_equal, OP.mult)
    settle(2)
    if not outer:
        pads(0, 1)
    share(0, flip(23, 24), "s0", e_off)
    take(0, (23, 24), "s0", e_off)
    g.remote_dma_fused([transfer(T.pic, 1024, 0, part, "ia", r, far, e_off)], local_sem=S.li)
    n_i += len(e_off)
    got = pick(0, (16, 24), 6)

    d0, d1 = 2 * slots[0] + 1, 2 * slots[-1]
    y1 = vec("ts", [t_1], col(13), T.k1[:, :], 1024.0, -512.0, OP.mult, OP.add)
    x1 = vec("ts", [], col(14), c, -4.0, float(base), OP.mult, OP.add)
    y4 = vec("ts", [], col(15), c, 1.0, 64.0, OP.is_lt, OP.mult)
    y2 = vec("ts", [y1], col(16), c, float(d0), col(13), OP.is_ge, OP.mult)
    x2 = vec("ts", [x1], col(17), T.k1[:, :], -3.0, col(14), OP.mult, OP.add)
    y5 = vec("ts", [y4], col(18), c, 15.0, col(15), OP.is_ge, OP.add)

    first = flip(17 if outer else 16, 23)
    early = flip(16 if outer else 15, 24)
    inner, nearwin, farwin = flip(16 if outer else 15, 25), flip(8, 24), flip(0, 16)
    note(0, first, got, early)
    both(0, first, early)
    note(0, flip(23, 24), got, inner)
    if outer:
        note(0, flip(16, 17), got, nearwin)
    look("ac", 0, *flip(23, 24), inner)
    share(1, first, "s1", e_all)
    share(1, flip(23, 24), "s2", e_all)

    y3 = vec("ts", [y2], col(19), c, float(d1), col(16), OP.is_le, OP.mult)
    t_b = vec("ts", [x2], col(9), c, 9.0, col(17), OP.is_lt, OP.mult)
    if wl is not None:
        x3 = vec("ts", [], col(20), c, 1.0, float(-wl), OP.is_lt, OP.mult)
        t_b = vec("tt", [t_b, x3], col(9), col(9), col(20), OP.add)
    if wh is not None:
        x3 = vec("ts", [], col(20), c, 8.0, float(32 - wh), OP.is_equal, OP.mult)
        y6 = vec("ts", [], col(21), c, 8.0, -64.0, OP.is_equal, OP.mult)
        t_b = vec("tt", [t_b, x3], col(9), col(9), col(20), OP.add)
        y5 = vec("tt", [y5, y6], col(18), col(18), col(21), OP.add)
    t_w4 = vec("tt", [y3, y5], col(10), col(19), col(18), OP.add)
    t_z4 = vec("ts", [t_zi, t_16, t_w4], T.z4[:, :], T.zio[:, :], col(4), col(10), OP.is_equal, OP.mult)

    if outer:
        spread(k_near)
        spread(k_far)
        settle(k_near)
        got = pick(0, flip(8, 16), 7)
        settle(k_far)
        got2 = pick(0, flip(2, 8), 6)
        note(0, flip(9, 16), got, nearwin)
        both(0, flip(9, 17), nearwin)
        share(1, flip(10, 17), "s3", e_all)
        note(0, flip(8, 9), got, farwin)
    mates_outer = 0 <= (mate + 1 if above else mate - 1) < n
    take(1, (17 if mates_outer else 16, 23), "s1", e_all)
    take(1, (23, 24), "s2", e_all)
    if mates_outer:
        take(1, (10, 17), "s3", e_all)

    p1, p2, p3 = flip(12 if outer else 16, 28), flip(4, 12), real(flip(28, 36))
    w1, w2, w3 = window(flip(10 if outer else 14, 30), 2), flip(2, 14), window(flip(26, 38), 2)
    g1 = pick(1, p1, 0)
    if outer:
        note(0, flip(2, 8), got2, farwin)
        both(0, flip(2, 9), farwin)
        g2 = pick(1, p2, 1)
    else:
        finish(1, w1)
    note(1, p1, g1, w1)
    both(1, p1, w1)
    if outer:
        note(1, p2, g2, w2)
        both(1, p2, w2)
        finish(1, w3)
    g.remote_dma_fused([transfer(T.pic, 1024, part, 1024, "h", r, [mate], e_all)], local_sem=S.li)
    n_i += len(e_all)
    passed = r + 2 if above else r - 2
    inside = [transfer(T.pic, 1024, 0, part, "ia", r, [mate], e_all)]
    n_i += len(e_all)
    if 0 <= passed < n:
        g.wait_ge(S[sname("ia", passed)], len(e_off))
        inside.append(transfer(T.pic, 1024, 0, part, "ia", passed, [mate], e_off))
        n_i += len(e_off)
    g.remote_dma_fused(inside, local_sem=S.li)

    x1 = window(flip(4 if outer else 12, 28), 4)
    x2, x3 = window(flip(20, 36), 4), window((8, 32), 8)
    q1, q2 = flip(8 if outer else 16, 24), real(flip(24, 32))
    g3 = pick(1, p3, 2)
    g4 = pick(2, q1, 3)
    if not outer:
        finish(2, x1)
    note(1, p3, g3, w3)
    both(1, p3, w3)
    g5 = pick(2, q2, 4)
    if outer:
        finish(2, x2)
    note(2, q1, g4, x1)
    both(2, (16, 24), x1)
    g6 = pick(3, (16, 24), 7)
    if outer:
        both(2, flip(8, 16), x1)
    note(2, q2, g5, x2)
    both(2, q2, x2)
    finish(3, x3)
    note(3, (16, 24), g6, x3)
    deps = toks(wrote[3], x3[0], x3[1]) + toks(listed[3], 16, 24) + [t_b]
    src = T.f3[:, x3[0] * 64:x3[1] * 64]
    v2 = act(deps, T.f4[:, 256:512], src.indirect(T.l3[:, 80:96]), RELU, bias=col(9))
    v1 = vec("ts", deps, T.f4[:, 0:256], src.indirect(T.l3[:, 64:80]), col(9), 0.0, OP.add, OP.max)

    need("pe", [v1, v2] + ps_free.get(5, []) + [t_z4])
    for k in range(16):
        tp = mark("pe", g.tensor.matmul(T.ps[:, 5 * 512:5 * 512 + 32], T.z4[:, 15 - k:143 - k], T.f4[:, k:512:16],
                                        k == 0, k == 15))
    t4 = vec("tc", [tp], T.l4[:, :], T.ps[:, 5 * 512:5 * 512 + 32])
    arrived = [(sname("ia", t), len(e_all) if t == mate else len(e_off)) for t in near]
    arrived += [(sname("h", t), len(e_all) if t == mate else len(e_off)) for t in near] + [("ldi", 16)]
    p0, p1 = slots[0] * 1024, slots[-1] * 1024 + 1024
    need("ve", arrived)
    need("ac", arrived)
    for h in range(2):
        a, src = 512 * h, T.pic[:, p0 + 512 * h:p1 - 512 + 512 * h]
        v1 = vec("tc", [t4], T.yo[:, a:a + 256], src.indirect(T.l4[:, 0:16]))
        v2 = act([t4], T.yo[:, a + 256:a + 512], src.indirect(T.l4[:, 16:32]), COPY)
        need("sy", [v1, v2])
        g.sync.dma_start(T.y[:, a:a + 512], T.yo[:, a:a + 512]).then_inc(S.sta, 16)
    g.sync.wait_ge(S.sta, 32)
    g.wait_ge(S.lv, n_v[0])
    g.wait_ge(S.li, n_i)
    for q in ("ve", "ac", "pe"):
        g.wait_ge(S[q], done[q])
    g.wait_ge(S.gp, done["gp"])
